import numpy as np
import ml_dtypes


def mxq(x, axis, fmt="e4m3"):
    dtype, down = {"e4m3": (ml_dtypes.float8_e4m3fn, 7), "e5m2": (ml_dtypes.float8_e5m2, 14)}[fmt]
    v = np.moveaxis(np.asarray(x, np.float32).astype(ml_dtypes.bfloat16).astype(np.float64), axis, -1)
    blocks = v.reshape(v.shape[:-1] + (-1, 32))
    amax = np.abs(blocks).max(-1, keepdims=True)
    byte = np.maximum(np.where(amax > 0, np.frexp(amax)[1] - 1 + 127, 0) - down, 1)
    scale = np.exp2(byte - 127.0)
    codes = (blocks / scale).astype(np.float32).astype(dtype).astype(np.float64)
    return np.moveaxis((codes * scale).reshape(v.shape), -1, axis)


WIDE = False


def mx_kscale(k):
    if not WIDE:
        return np.ones(k)
    levels = np.array([10, -10, 5, -5, 0])
    if k % 512:
        return np.exp2(np.random.permutation(np.resize(levels, k // 32))).repeat(32)
    a = np.empty((k // 512, 16))
    for p in range(k // 512):
        a[p, :8] = np.random.permutation(np.resize(levels, 8))
        for g in range(8):
            far = levels[np.abs(levels - a[p, g]) >= 10]
            a[p, g + 8] = far[np.random.randint(len(far))]
    return np.exp2(a.ravel()).repeat(32)


def f64(x):
    return np.asarray(x).astype(np.float64)


def striped(idx):
    return np.tile(idx.reshape(-1, 16).T, (8, 1)).astype(np.uint16)


def unstriped(offs):
    return offs[:16].T.reshape(-1).astype(np.int64)


E2M1 = np.array([0.0, 0.5, 1.0, 1.5, 2.0, 3.0, 4.0, 6.0, -0.0, -0.5, -1.0, -1.5, -2.0, -3.0, -4.0, -6.0])


def pack_weight(w, fmt):
    k, n = w.shape
    w = f64(np.asarray(w, np.float32).astype(ml_dtypes.bfloat16)).reshape(k // 32, 32, n)
    amax = np.abs(w).max(1)
    if fmt == "e4m3":
        byte = np.frexp(amax)[1] - 1 + 127 - 7
    else:
        mant, ex = np.frexp(amax / 6.0)
        byte = np.where(mant > 0.5, ex, ex - 1) + 127
    byte = np.clip(np.where(amax > 0, byte, 1), 1, 254)
    scaled = (w * np.exp2(127.0 - byte)[:, None, :]).reshape(k, n).astype(np.float32)
    by_word = np.ascontiguousarray(scaled.reshape(k // 512, 128, 4, n).transpose(0, 1, 3, 2))
    if fmt == "e4m3":
        words = by_word.astype(ml_dtypes.float8_e4m3fn).view(np.uint8)
    else:
        c = by_word.astype(ml_dtypes.float4_e2m1fn).view(np.uint8) & 0xF
        words = (c[..., 0::2] | (c[..., 1::2] << 4)).reshape(k // 512, 128, 2 * n)
    return np.ascontiguousarray(words), np.ascontiguousarray(byte.astype(np.uint8).reshape(k // 512, 16, n))


def unpack_weight(words, scales, fmt):
    g, _, n = scales.shape
    words = np.ascontiguousarray(words).reshape(g, 128, n, -1)
    if fmt == "e4m3":
        vals = words.view(ml_dtypes.float8_e4m3fn).astype(np.float64)
    else:
        nib = np.empty((g, 128, n, 4), np.uint8)
        nib[..., 0::2] = words & 0xF
        nib[..., 1::2] = words >> 4
        vals = E2M1[nib]
    vals = vals * np.repeat(np.exp2(scales.astype(np.float64) - 127.0), 8, axis=1)[..., None]
    return vals.transpose(0, 1, 3, 2).reshape(g * 512, n)


def gelu(v):
    return 0.5 * v * (1.0 + np.tanh(np.sqrt(2.0 / np.pi) * (v + 0.044715 * v**3)))


K, T, E, C, H, N = 512, 3072, 8, 256, 512, 128


def by_expert(wq, xq):
    return np.concatenate([wq[e].T @ xq[:, e * C:(e + 1) * C] for e in range(E)], axis=1)


def setup_inputs():
    n = np.random.standard_normal
    s = mx_kscale(K)[:, None]
    u = mx_kscale(H)
    w1 = [pack_weight(m, "e2m1") for m in n((E, K, H)) / np.sqrt(K) / s[None]]
    w3 = [pack_weight(m, "e2m1") for m in n((E, K, H)) / np.sqrt(K) / s[None] * u[None, None, :]]
    w2 = [pack_weight(m, "e2m1") for m in n((E, H, N)) / np.sqrt(H) / u[None, :, None]]
    return {
        "xT": (n((K, T)) * s).astype(np.float32),
        "xr": n((N, T)).astype(np.float32),
        "w1_words": np.stack([m[0] for m in w1]),
        "w1_scales": np.stack([m[1] for m in w1]),
        "w3_words": np.stack([m[0] for m in w3]),
        "w3_scales": np.stack([m[1] for m in w3]),
        "w2_words": np.stack([m[0] for m in w2]),
        "w2_scales": np.stack([m[1] for m in w2]),
        "gate": np.tile(np.random.uniform(0.2, 1.0, E * C), (N, 1)).astype(np.float32),
        "offs": striped(np.random.permutation(T)[:E * C]),
    }


def reference(xT, xr, w1_words, w1_scales, w3_words, w3_scales, w2_words, w2_scales, gate, offs):
    idx = unstriped(offs)
    w1 = np.stack([unpack_weight(w1_words[e], w1_scales[e], "e2m1") for e in range(E)])
    w3 = np.stack([unpack_weight(w3_words[e], w3_scales[e], "e2m1") for e in range(E)])
    w2 = np.stack([unpack_weight(w2_words[e], w2_scales[e], "e2m1") for e in range(E)])
    xq = mxq(f64(xT)[:, idx], 0, "e4m3")
    h = gelu(by_expert(w1, xq))
    h = h * by_expert(w3, xq)
    y = by_expert(w2, mxq(h, 0, "e4m3"))
    out = f64(xr).copy()
    out[:, idx] += f64(gate) * y
    return out

@@ -1,0 +1,253 @@
+from contextlib import ExitStack
+
+import concourse.mybir as mybir
+from concourse.masks import make_identity
+
+F32 = mybir.dt.float32
+BF16 = mybir.dt.bfloat16
+I32 = mybir.dt.int32
+U32 = mybir.dt.uint32
+U16 = mybir.dt.uint16
+U8 = mybir.dt.uint8
+FP8X4 = mybir.dt.float8_e4m3fn_x4
+FP4X4 = mybir.dt.float4_e2m1fn_x4
+GELU = mybir.ActivationFunctionType.Gelu_apprx_tanh
+MULT = mybir.AluOpType.mult
+ADD = mybir.AluOpType.add
+
+P = 128
+K, T, E, C, H, N = 512, 3072, 8, 256, 512, 128
+S = E * C
+SLICE = 512
+FLOPS = 2 * S * (2 * K * H + H * N)
+
+
+def tile_moe_res_glu_gelu_kernel(
+    tc, xT, xr, w1_words, w1_scales, w3_words, w3_scales, w2_words, w2_scales, gate, offs, out
+):
+    nc = tc.nc
+    x_rows = xT.rearrange("(p j) t -> p j t", j=4)
+    slices = S // SLICE
+
+    with ExitStack() as ctx:
+        keep = ctx.enter_context(tc.tile_pool(name="keep", bufs=1))
+        raw_pool = ctx.enter_context(tc.tile_pool(name="raw", bufs=1))
+        slot_pool = ctx.enter_context(tc.tile_pool(name="slots", bufs=4))
+        work = ctx.enter_context(tc.tile_pool(name="work", bufs=4))
+        act_pool = ctx.enter_context(tc.tile_pool(name="acts", bufs=6))
+        psum = ctx.enter_context(tc.psum_pool(name="psum", bufs=8))
+
+        offsets = keep.tile([P, S // 16], U16, name="offsets")
+        pairs = [keep.tile([P, 2 * T], BF16, name=f"pairs{u}", align_bytes=64) for u in range(2)]
+        w1_codes = keep.tile([P, E * 2 * H], U8, name="w1_codes", align_bytes=64)
+        w3_codes = keep.tile([P, E * 2 * H], U8, name="w3_codes", align_bytes=64)
+        w2_codes = keep.tile([P, E * 2 * N], U8, name="w2_codes", align_bytes=64)
+        w1_plane = keep.tile([P, E * H], U8, name="w1_plane", align_bytes=64)
+        w3_plane = keep.tile([P, E * H], U8, name="w3_plane", align_bytes=64)
+        w2_plane = keep.tile([P, E * N], U8, name="w2_plane", align_bytes=64)
+        gates = keep.tile([P, S], F32, name="gates")
+        residual = keep.tile([P, T], F32, name="residual")
+        scattered = keep.tile([P, T], F32, name="scattered")
+        identity = keep.tile([P, P], F32, name="identity")
+        warm = keep.tile([P, 1], F32, name="warm")
+
+        nc.vector.memset(warm[:], 0.0)
+        nc.vector.memset(scattered[:], 0.0)
+        nc.scalar.activation(warm[:], warm[:], GELU)
+        for plane in (w1_plane, w3_plane, w2_plane):
+            nc.gpsimd.memset(plane[:].bitcast(I32), 0)
+        make_identity(nc, identity[:])
+
+        def load_and_cast(u, c0, c1, split):
+            width = c1 - c0
+            raw = raw_pool.tile([P, 2, width], F32, name=f"raw{u}_{c0}")
+            nc.sync.dma_start(out=raw[:], in_=x_rows[:, 2 * u : 2 * u + 2, c0:c1])
+            dst = pairs[u][:].rearrange("p (t e) -> p t e", e=2)
+            source = raw[:].rearrange("p e t -> p t e")
+            if split > 0:
+                nc.scalar.copy(out=dst[:, c0 : c0 + split, :], in_=source[:, 0:split, :])
+            if split < width:
+                nc.vector.tensor_copy(out=dst[:, c0 + split : c1, :], in_=source[:, split:width, :])
+
+        def gather(u, first, last):
+            nc.vector.tensor_copy(
+                gathered[:, 2 * (u * S + first) : 2 * (u * S + last)].bitcast(U32),
+                pairs[u][:].bitcast(U32).indirect(offsets[:, first // 16 : last // 16]),
+            )
+
+        load_and_cast(0, 0, 2048, 896)
+        nc.sync.dma_start(offsets[:], offs)
+        load_and_cast(0, 2048, 3072, 384)
+        gathered = keep.tile([P, slices * 4 * SLICE], BF16, name="gathered", align_bytes=64)
+        for first in range(0, S, S // 2):
+            gather(0, first, first + S // 2)
+        load_and_cast(1, 0, 1024, 1024)
+        load_and_cast(1, 1024, 2048, 1024)
+        load_and_cast(1, 2048, 2816, 0)
+        load_and_cast(1, 2816, 3072, 0)
+
+        def load_scales(plane, scales, e0, e1):
+            wide = scales.shape[3]
+            rows = scales[e0:e1].rearrange("e s (q r) i -> r q (e s) i", r=4)
+            for r in range(4):
+                nc.sync.dma_start(
+                    out=plane[r:P:32, e0 * wide : e1 * wide].bitcast(I32).rearrange("q (e i) -> q e i", e=e1 - e0),
+                    in_=rows[r].bitcast(I32),
+                )
+
+        def load_words(codes, words, e0, e1):
+            wide = words.shape[3]
+            nc.sync.dma_start(
+                out=codes[:, e0 * wide : e1 * wide].bitcast(I32).rearrange("p (e b) -> p e b", e=e1 - e0),
+                in_=words[e0:e1].rearrange("e s p b -> p (e s) b").bitcast(I32),
+            )
+
+        load_scales(w1_plane, w1_scales, 0, 2)
+        load_words(w1_codes, w1_words, 0, 2)
+        load_scales(w3_plane, w3_scales, 0, 2)
+        load_words(w3_codes, w3_words, 0, 2)
+        load_words(w1_codes, w1_words, 2, 4)
+        load_words(w3_codes, w3_words, 2, 4)
+        load_scales(w1_plane, w1_scales, 2, E)
+        load_scales(w3_plane, w3_scales, 2, E)
+        load_scales(w2_plane, w2_scales, 0, E)
+        load_words(w2_codes, w2_words, 0, E)
+        nc.sync.dma_start(out=gates[:], in_=gate)
+        load_words(w1_codes, w1_words, 4, E)
+        load_words(w3_codes, w3_words, 4, E)
+        nc.sync.dma_start(out=residual[:], in_=xr)
+
+        x_codes = [slot_pool.tile([P, SLICE], U32, name="x_codes", align_bytes=64) for s in range(slices)]
+        x_scales = [slot_pool.tile([P, SLICE], U8, name="x_scales", align_bytes=64) for s in range(slices)]
+        a_banks, b_banks, acts, hiddens, turned, h_grouped, h_codes, h_scales, y_banks, results = ({} for i in range(10))
+
+        by_pair = gathered[:].bitcast(F32).rearrange("p (u t) -> p t u", u=2)
+
+        def quantise_tokens(e):
+            s, at = e // 2, (e % 2) * C
+            width = C if e < 4 else SLICE
+            if e < 2:
+                place = 2 * S + 2 * (e + 2) * SLICE
+                grouped = gathered[:, place : place + 4 * width]
+            else:
+                grouped = slot_pool.tile([P, 4 * width], BF16, name="grouped", align_bytes=64)[:]
+            nc.scalar.copy(
+                out=grouped.bitcast(F32).rearrange("p (t u) -> p t u", u=2),
+                in_=by_pair[:, e * C : e * C + width, :],
+            )
+            nc.vector.quantize_mx(
+                out=x_codes[s][:, at : at + width].bitcast(FP8X4),
+                scales=x_scales[s][:, at : at + width],
+                in_=grouped,
+            )
+
+        def first_products(c):
+            e, s, at = c // 2, c // 4, (c % 4) * P
+            for banks, codes, plane in ((a_banks, w1_codes, w1_plane), (b_banks, w3_codes, w3_plane)):
+                banks[c] = psum.tile([P, H], F32, name="bank")
+                nc.tensor.matmul_mx(
+                    out=banks[c][:],
+                    lhsT=x_codes[s][:, at : at + P].bitcast(FP8X4),
+                    lhsT_scale=x_scales[s][:, at : at + P],
+                    rhs=codes[:, e * 2 * H : (e + 1) * 2 * H].bitcast(FP4X4),
+                    rhs_scale=plane[:, e * H : (e + 1) * H],
+                    start=True,
+                    stop=True,
+                )
+
+        def activate(c):
+            acts[c] = act_pool.tile([P, H], F32, name="act")
+            nc.scalar.activation(
+                acts[c][:].rearrange("s (u p e) -> s u p e", u=2, e=2),
+                a_banks[c][:].rearrange("s (p u e) -> s u p e", u=2, e=2),
+                GELU,
+            )
+
+        def multiply(c):
+            hiddens[c] = work.tile([P, H], BF16, name="hidden", align_bytes=64)
+            nc.vector.tensor_tensor(
+                hiddens[c][:].rearrange("s (u p e) -> s u p e", u=2, e=2),
+                b_banks[c][:].rearrange("s (p u e) -> s u p e", u=2, e=2),
+                acts[c][:].rearrange("s (u p e) -> s u p e", u=2, e=2),
+                MULT,
+            )
+
+        def turn(c):
+            if c % 2 == 0:
+                turned[c // 2] = psum.tile([P, 4 * P], F32, name="bank")
+            words = hiddens[c][:].bitcast(F32)
+            for u in range(2):
+                place = (2 * (c % 2) + u) * P
+                nc.tensor.transpose(turned[c // 2][:, place : place + P], words[:, u * P : (u + 1) * P], identity[:])
+
+        def group_hidden(e):
+            h_grouped[e] = work.tile([P, 4 * C], BF16, name="h_grouped", align_bytes=64)
+            nc.scalar.copy(
+                out=h_grouped[e][:].bitcast(F32).rearrange("p (c r u) -> p c r u", c=2, u=2),
+                in_=turned[e][:].rearrange("p (c u r) -> p c r u", c=2, u=2),
+            )
+
+        def quantise_hidden(e):
+            h_codes[e] = work.tile([P, C], U32, name="h_codes", align_bytes=64)
+            h_scales[e] = work.tile([P, C], U8, name="h_scales", align_bytes=64)
+            nc.vector.quantize_mx(out=h_codes[e][:].bitcast(FP8X4), scales=h_scales[e][:], in_=h_grouped[e][:])
+
+        def second_product(e):
+            if e % 2 == 0:
+                y_banks[e // 2] = psum.tile([P, SLICE], F32, name="bank")
+            nc.tensor.matmul_mx(
+                out=y_banks[e // 2][:, (e % 2) * C : (e % 2 + 1) * C],
+                lhsT=w2_codes[:, e * 2 * N : (e + 1) * 2 * N].bitcast(FP4X4),
+                lhsT_scale=w2_plane[:, e * N : (e + 1) * N],
+                rhs=h_codes[e][:].bitcast(FP8X4),
+                rhs_scale=h_scales[e][:],
+                start=True,
+                stop=True,
+            )
+
+        def collect(s):
+            results[s] = work.tile([P, SLICE], F32, name="results")
+            nc.scalar.copy(out=results[s][:], in_=y_banks[s][:])
+
+        def scatter(s):
+            nc.vector.tensor_tensor(
+                scattered[:].indirect(offsets[:, s * (SLICE // 16) : (s + 1) * (SLICE // 16)]),
+                results[s][:],
+                gates[:, s * SLICE : (s + 1) * SLICE],
+                MULT,
+            )
+
+        gather(1, 0 * SLICE, 1 * SLICE)
+        gather(1, 1 * SLICE, 2 * SLICE)
+        quantise_tokens(0)
+        quantise_tokens(1)
+        gather(1, 2 * SLICE, 3 * SLICE)
+        gather(1, 3 * SLICE, 4 * SLICE)
+        chunks = S // P
+        scatter_at = (12, 14, 18, 23)
+        for c in range(-3, max(scatter_at) + 1):
+            if c in (-1, 1, 3, 7):
+                quantise_tokens((c + 5) // 2)
+            if 0 <= c + 3 < chunks:
+                first_products(c + 3)
+            if 0 <= c + 1 < chunks:
+                activate(c + 1)
+            if 0 <= c < chunks:
+                multiply(c)
+            if 0 <= c - 1 < chunks:
+                turn(c - 1)
+            if (c - 1) % 2 == 1 and 0 < c - 1 < chunks:
+                group_hidden((c - 1) // 2)
+            if (c - 2) % 2 == 1 and 0 < c - 2 < chunks:
+                quantise_hidden((c - 2) // 2)
+            if (c - 4) % 2 == 1 and 0 < c - 4 < chunks:
+                second_product((c - 4) // 2)
+            if (c - 5) % 4 == 3 and 0 < c - 5 < chunks:
+                collect((c - 5) // 4)
+            if c in scatter_at:
+                scatter(scatter_at.index(c))
+
+        bounds = [0, 640, 1280, 1920, 2560, T]
+        for c0, c1 in zip(bounds[:-1], bounds[1:]):
+            nc.vector.tensor_tensor(residual[:, c0:c1], residual[:, c0:c1], scattered[:, c0:c1], ADD)
+            nc.sync.dma_start(out=out[:, c0:c1], in_=residual[:, c0:c1])

@@ -12,6 +12,7 @@ U8 = mybir.dt.uint8
 FP8X4 = mybir.dt.float8_e4m3fn_x4
 FP4X4 = mybir.dt.float4_e2m1fn_x4
 GELU = mybir.ActivationFunctionType.Gelu_apprx_tanh
+COPY = mybir.ActivationFunctionType.Copy
 MULT = mybir.AluOpType.mult
 ADD = mybir.AluOpType.add
 
@@ -19,6 +20,9 @@ P = 128
 K, T, E, C, H, N = 512, 3072, 8, 256, 512, 128
 S = E * C
 SLICE = 512
+CUTS = (0, 4, 7, 10, 13, 16)
+HELD_BY = (4, 10, 14)
+LATE_AFTER = (0, 3)
 FLOPS = 2 * S * (2 * K * H + H * N)
 
 
@@ -38,7 +42,12 @@ def tile_moe_res_glu_gelu_kernel(
         psum = ctx.enter_context(tc.psum_pool(name="psum", bufs=8))
 
         offsets = keep.tile([P, S // 16], U16, name="offsets")
-        pairs = [keep.tile([P, 2 * T], BF16, name=f"pairs{u}", align_bytes=64) for u in range(2)]
+        pairs = keep.tile([P, 2 * T + 4 * SLICE], BF16, name="pairs", align_bytes=64)
+        singles = {j: keep.tile([P, T + (j - 2) * 2 * H], BF16, name=f"single{j}", align_bytes=64) for j in (2, 3)}
+        grouped = [pairs[:, 2 * T : 2 * T + 4 * SLICE]]
+        grouped.extend(
+            keep.tile([P, 4 * SLICE], BF16, name=f"grouped{s}", align_bytes=64)[:] for s in range(1, slices)
+        )
         w1_codes = keep.tile([P, E * 2 * H], U8, name="w1_codes", align_bytes=64)
         w3_codes = keep.tile([P, E * 2 * H], U8, name="w3_codes", align_bytes=64)
         w2_codes = keep.tile([P, E * 2 * N], U8, name="w2_codes", align_bytes=64)
@@ -58,33 +67,50 @@ def tile_moe_res_glu_gelu_kernel(
             nc.gpsimd.memset(plane[:].bitcast(I32), 0)
         make_identity(nc, identity[:])
 
-        def load_and_cast(u, c0, c1, split):
-            width = c1 - c0
-            raw = raw_pool.tile([P, 2, width], F32, name=f"raw{u}_{c0}")
-            nc.sync.dma_start(out=raw[:], in_=x_rows[:, 2 * u : 2 * u + 2, c0:c1])
-            dst = pairs[u][:].rearrange("p (t e) -> p t e", e=2)
-            source = raw[:].rearrange("p e t -> p t e")
-            if split > 0:
-                nc.scalar.copy(out=dst[:, c0 : c0 + split, :], in_=source[:, 0:split, :])
-            if split < width:
-                nc.vector.tensor_copy(out=dst[:, c0 + split : c1, :], in_=source[:, split:width, :])
+        def load_pairs(c0, c1):
+            raw = raw_pool.tile([P, 2, c1 - c0], F32, name=f"raw_pairs{c0}")
+            nc.sync.dma_start(out=raw[:], in_=x_rows[:, 0:2, c0:c1])
+            dst = pairs[:, 0 : 2 * T].rearrange("p (t e) -> p t e", e=2)
+            nc.vector.tensor_copy(out=dst[:, c0:c1, :], in_=raw[:].rearrange("p e t -> p t e"))
 
-        def gather(u, first, last):
+        def load_single(j, c0, c1):
+            raw = raw_pool.tile([P, c1 - c0], F32, name=f"raw{j}_{c0}")
+            nc.sync.dma_start(out=raw[:], in_=x_rows[:, j, c0:c1])
+            if j == 2:
+                nc.vector.tensor_copy(out=singles[j][:, c0:c1], in_=raw[:])
+            else:
+                nc.scalar.copy(out=singles[j][:, c0:c1], in_=raw[:])
+
+        def entries(s):
+            return offsets[:, s * (SLICE // 16) : (s + 1) * (SLICE // 16)]
+
+        def gather_pairs(s):
             nc.vector.tensor_copy(
-                gathered[:, 2 * (u * S + first) : 2 * (u * S + last)].bitcast(U32),
-                pairs[u][:].bitcast(U32).indirect(offsets[:, first // 16 : last // 16]),
+                grouped[s].bitcast(U32).rearrange("p (t u) -> p t u", u=2)[:, :, 0],
+                pairs[:].bitcast(U32)[:, 0 : T + (s // 3) * 2 * SLICE].indirect(entries(s)),
             )
 
-        load_and_cast(0, 0, 2048, 896)
+        def gather_single(j, s):
+            nc.scalar.activation(
+                grouped[s].rearrange("p (t d) -> p t d", d=4)[:, :, j],
+                singles[j][:, 0 : T + (16 if j == 3 and s >= 2 else 0)].indirect(entries(s)),
+                COPY,
+            )
+
+        load_single(2, 0, 2048)
         nc.sync.dma_start(offsets[:], offs)
-        load_and_cast(0, 2048, 3072, 384)
-        gathered = keep.tile([P, slices * 4 * SLICE], BF16, name="gathered", align_bytes=64)
-        for first in range(0, S, S // 2):
-            gather(0, first, first + S // 2)
-        load_and_cast(1, 0, 1024, 1024)
-        load_and_cast(1, 1024, 2048, 1024)
-        load_and_cast(1, 2048, 2816, 0)
-        load_and_cast(1, 2816, 3072, 0)
+        load_single(2, 2048, T)
+        for s in range(slices):
+            gather_single(2, s)
+        load_pairs(0, 1408)
+        load_pairs(1408, 2816)
+        load_pairs(2816, T)
+        for s in range(slices - 1):
+            gather_pairs(s)
+        load_single(3, 0, 768)
+        load_single(3, 768, 1792)
+        load_single(3, 1792, 2688)
+        load_single(3, 2688, 3072)
 
         def load_scales(plane, scales, e0, e1):
             wide = scales.shape[3]
@@ -102,43 +128,30 @@ def tile_moe_res_glu_gelu_kernel(
                 in_=words[e0:e1].rearrange("e s p b -> p (e s) b").bitcast(I32),
             )
 
-        load_scales(w1_plane, w1_scales, 0, 2)
+        load_scales(w1_plane, w1_scales, 0, E)
         load_words(w1_codes, w1_words, 0, 2)
-        load_scales(w3_plane, w3_scales, 0, 2)
+        load_scales(w3_plane, w3_scales, 0, E)
         load_words(w3_codes, w3_words, 0, 2)
         load_words(w1_codes, w1_words, 2, 4)
         load_words(w3_codes, w3_words, 2, 4)
-        load_scales(w1_plane, w1_scales, 2, E)
-        load_scales(w3_plane, w3_scales, 2, E)
         load_scales(w2_plane, w2_scales, 0, E)
         load_words(w2_codes, w2_words, 0, E)
-        nc.sync.dma_start(out=gates[:], in_=gate)
+        nc.sync.dma_start(out=gates[:, 0 : S // 2], in_=gate[:, 0 : S // 2])
         load_words(w1_codes, w1_words, 4, E)
         load_words(w3_codes, w3_words, 4, E)
+        nc.sync.dma_start(out=gates[:, S // 2 : S], in_=gate[:, S // 2 : S])
         nc.sync.dma_start(out=residual[:], in_=xr)
 
         x_codes = [slot_pool.tile([P, SLICE], U32, name="x_codes", align_bytes=64) for s in range(slices)]
         x_scales = [slot_pool.tile([P, SLICE], U8, name="x_scales", align_bytes=64) for s in range(slices)]
-        a_banks, b_banks, acts, hiddens, turned, h_grouped, h_codes, h_scales, y_banks, results = ({} for i in range(10))
+        a_banks, b_banks, acts, hiddens, turned, h_grouped, h_codes, h_scales, y_banks = ({} for i in range(9))
+        results = [keep.tile([P, H], F32, name=f"results{k}") for k in range(len(CUTS) - 1)]
 
-        by_pair = gathered[:].bitcast(F32).rearrange("p (u t) -> p t u", u=2)
-
-        def quantise_tokens(e):
-            s, at = e // 2, (e % 2) * C
-            width = C if e < 4 else SLICE
-            if e < 2:
-                place = 2 * S + 2 * (e + 2) * SLICE
-                grouped = gathered[:, place : place + 4 * width]
-            else:
-                grouped = slot_pool.tile([P, 4 * width], BF16, name="grouped", align_bytes=64)[:]
-            nc.scalar.copy(
-                out=grouped.bitcast(F32).rearrange("p (t u) -> p t u", u=2),
-                in_=by_pair[:, e * C : e * C + width, :],
-            )
+        def quantise_tokens(s, first, last):
             nc.vector.quantize_mx(
-                out=x_codes[s][:, at : at + width].bitcast(FP8X4),
-                scales=x_scales[s][:, at : at + width],
-                in_=grouped,
+                out=x_codes[s][:, first:last].bitcast(FP8X4),
+                scales=x_scales[s][:, first:last],
+                in_=grouped[s][:, 4 * first : 4 * last],
             )
 
         def first_products(c):
@@ -156,9 +169,12 @@ def tile_moe_res_glu_gelu_kernel(
                 )
 
         def activate(c):
-            acts[c] = act_pool.tile([P, H], F32, name="act")
+            if c in HELD_BY:
+                acts[c] = results[HELD_BY.index(c)][:]
+            else:
+                acts[c] = act_pool.tile([P, H], F32, name="act")[:]
             nc.scalar.activation(
-                acts[c][:].rearrange("s (u p e) -> s u p e", u=2, e=2),
+                acts[c].rearrange("s (u p e) -> s u p e", u=2, e=2),
                 a_banks[c][:].rearrange("s (p u e) -> s u p e", u=2, e=2),
                 GELU,
             )
@@ -168,7 +184,7 @@ def tile_moe_res_glu_gelu_kernel(
             nc.vector.tensor_tensor(
                 hiddens[c][:].rearrange("s (u p e) -> s u p e", u=2, e=2),
                 b_banks[c][:].rearrange("s (p u e) -> s u p e", u=2, e=2),
-                acts[c][:].rearrange("s (u p e) -> s u p e", u=2, e=2),
+                acts[c].rearrange("s (u p e) -> s u p e", u=2, e=2),
                 MULT,
             )
 
@@ -181,71 +197,91 @@ def tile_moe_res_glu_gelu_kernel(
                 nc.tensor.transpose(turned[c // 2][:, place : place + P], words[:, u * P : (u + 1) * P], identity[:])
 
         def group_hidden(e):
-            h_grouped[e] = work.tile([P, 4 * C], BF16, name="h_grouped", align_bytes=64)
+            if e in LATE_AFTER:
+                h_grouped[e] = singles[3][:, T : T + 4 * C]
+            else:
+                h_grouped[e] = work.tile([P, 4 * C], BF16, name="h_grouped", align_bytes=64)[:]
             nc.scalar.copy(
-                out=h_grouped[e][:].bitcast(F32).rearrange("p (c r u) -> p c r u", c=2, u=2),
+                out=h_grouped[e].bitcast(F32).rearrange("p (c r u) -> p c r u", c=2, u=2),
                 in_=turned[e][:].rearrange("p (c u r) -> p c r u", c=2, u=2),
             )
 
         def quantise_hidden(e):
             h_codes[e] = work.tile([P, C], U32, name="h_codes", align_bytes=64)
             h_scales[e] = work.tile([P, C], U8, name="h_scales", align_bytes=64)
-            nc.vector.quantize_mx(out=h_codes[e][:].bitcast(FP8X4), scales=h_scales[e][:], in_=h_grouped[e][:])
+            nc.vector.quantize_mx(out=h_codes[e][:].bitcast(FP8X4), scales=h_scales[e][:], in_=h_grouped[e])
 
         def second_product(e):
-            if e % 2 == 0:
-                y_banks[e // 2] = psum.tile([P, SLICE], F32, name="bank")
-            nc.tensor.matmul_mx(
-                out=y_banks[e // 2][:, (e % 2) * C : (e % 2 + 1) * C],
-                lhsT=w2_codes[:, e * 2 * N : (e + 1) * 2 * N].bitcast(FP4X4),
-                lhsT_scale=w2_plane[:, e * N : (e + 1) * N],
-                rhs=h_codes[e][:].bitcast(FP8X4),
-                rhs_scale=h_scales[e][:],
-                start=True,
-                stop=True,
-            )
+            for k in range(len(CUTS) - 1):
+                first, last = max(CUTS[k], 2 * e), min(CUTS[k + 1], 2 * e + 2)
+                if first < last:
+                    if first == CUTS[k]:
+                        y_banks[k] = psum.tile([P, SLICE], F32, name="bank")
+                    mine = slice((first - 2 * e) * P, (last - 2 * e) * P)
+                    nc.tensor.matmul_mx(
+                        out=y_banks[k][:, (first - CUTS[k]) * P : (last - CUTS[k]) * P],
+                        lhsT=w2_codes[:, e * 2 * N : (e + 1) * 2 * N].bitcast(FP4X4),
+                        lhsT_scale=w2_plane[:, e * N : (e + 1) * N],
+                        rhs=h_codes[e][:, mine].bitcast(FP8X4),
+                        rhs_scale=h_scales[e][:, mine],
+                        start=True,
+                        stop=True,
+                    )
 
-        def collect(s):
-            results[s] = work.tile([P, SLICE], F32, name="results")
-            nc.scalar.copy(out=results[s][:], in_=y_banks[s][:])
+        def collect(k):
+            width = (CUTS[k + 1] - CUTS[k]) * P
+            nc.scalar.copy(out=results[k][:, 0:width], in_=y_banks[k][:, 0:width])
 
-        def scatter(s):
+        def scatter(k):
+            first, last = CUTS[k] * P, CUTS[k + 1] * P
             nc.vector.tensor_tensor(
-                scattered[:].indirect(offsets[:, s * (SLICE // 16) : (s + 1) * (SLICE // 16)]),
-                results[s][:],
-                gates[:, s * SLICE : (s + 1) * SLICE],
+                scattered[:].indirect(offsets[:, first // 16 : last // 16]),
+                results[k][:, 0 : last - first],
+                gates[:, first:last],
                 MULT,
             )
 
-        gather(1, 0 * SLICE, 1 * SLICE)
-        gather(1, 1 * SLICE, 2 * SLICE)
-        quantise_tokens(0)
-        quantise_tokens(1)
-        gather(1, 2 * SLICE, 3 * SLICE)
-        gather(1, 3 * SLICE, 4 * SLICE)
+        def gate_chunk(c):
+            activate(c)
+            multiply(c)
+
+        def turn_expert(e):
+            turn(2 * e)
+            turn(2 * e + 1)
+
+        def second_layer(e):
+            group_hidden(e)
+            quantise_hidden(e)
+            second_product(e)
+
+        gather_single(3, 0)
+        quantise_tokens(0, 0, C)
+        quantise_tokens(0, C, SLICE)
+        gather_pairs(3)
+        gather_single(3, 1)
+        quantise_tokens(1, 0, SLICE)
         chunks = S // P
-        scatter_at = (12, 14, 18, 23)
-        for c in range(-3, max(scatter_at) + 1):
-            if c in (-1, 1, 3, 7):
-                quantise_tokens((c + 5) // 2)
-            if 0 <= c + 3 < chunks:
+        for c in range(3):
+            first_products(c)
+        for c in range(chunks + 2):
+            if c < chunks:
+                gate_chunk(c)
+            if c % 2 == 1 and c < chunks:
+                turn_expert(c // 2)
+            if c % 2 == 1 and c >= 3:
+                second_layer((c - 3) // 2)
+            if c - 3 in (2 * e for e in LATE_AFTER):
+                late = 2 + LATE_AFTER.index((c - 3) // 2)
+                gather_single(3, late)
+                quantise_tokens(late, 0, SLICE)
+            if c + 3 < chunks:
                 first_products(c + 3)
-            if 0 <= c + 1 < chunks:
-                activate(c + 1)
-            if 0 <= c < chunks:
-                multiply(c)
-            if 0 <= c - 1 < chunks:
-                turn(c - 1)
-            if (c - 1) % 2 == 1 and 0 < c - 1 < chunks:
-                group_hidden((c - 1) // 2)
-            if (c - 2) % 2 == 1 and 0 < c - 2 < chunks:
-                quantise_hidden((c - 2) // 2)
-            if (c - 4) % 2 == 1 and 0 < c - 4 < chunks:
-                second_product((c - 4) // 2)
-            if (c - 5) % 4 == 3 and 0 < c - 5 < chunks:
-                collect((c - 5) // 4)
-            if c in scatter_at:
-                scatter(scatter_at.index(c))
+            if c - 1 in HELD_BY:
+                collect(HELD_BY.index(c - 1))
+                scatter(HELD_BY.index(c - 1))
+        for k in range(len(HELD_BY), len(CUTS) - 1):
+            collect(k)
+            scatter(k)
 
         bounds = [0, 640, 1280, 1920, 2560, T]
         for c0, c1 in zip(bounds[:-1], bounds[1:]):

@@ -22,7 +22,8 @@ S = E * C
 SLICE = 512
 CUTS = (0, 4, 7, 10, 13, 16)
 HELD_BY = (4, 10, 14)
-LATE_AFTER = (0, 3)
+LATE_AFTER = (3,)
+RUN = 4
 FLOPS = 2 * S * (2 * K * H + H * N)
 
 
@@ -51,8 +52,8 @@ def tile_moe_res_glu_gelu_kernel(
         w1_codes = keep.tile([P, E * 2 * H], U8, name="w1_codes", align_bytes=64)
         w3_codes = keep.tile([P, E * 2 * H], U8, name="w3_codes", align_bytes=64)
         w2_codes = keep.tile([P, E * 2 * N], U8, name="w2_codes", align_bytes=64)
-        w1_plane = keep.tile([P, E * H], U8, name="w1_plane", align_bytes=64)
-        w3_plane = keep.tile([P, E * H], U8, name="w3_plane", align_bytes=64)
+        w1_planes = [keep.tile([P, RUN * H], U8, name=f"w1_plane{r}", align_bytes=64) for r in range(E // RUN)]
+        w3_planes = [keep.tile([P, RUN * H], U8, name=f"w3_plane{r}", align_bytes=64) for r in range(E // RUN)]
         w2_plane = keep.tile([P, E * N], U8, name="w2_plane", align_bytes=64)
         gates = keep.tile([P, S], F32, name="gates")
         residual = keep.tile([P, T], F32, name="residual")
@@ -61,10 +62,10 @@ def tile_moe_res_glu_gelu_kernel(
         warm = keep.tile([P, 1], F32, name="warm")
 
         nc.vector.memset(warm[:], 0.0)
-        nc.vector.memset(scattered[:], 0.0)
         nc.scalar.activation(warm[:], warm[:], GELU)
-        for plane in (w1_plane, w3_plane, w2_plane):
-            nc.gpsimd.memset(plane[:].bitcast(I32), 0)
+        for plane in (w1_planes[0], w3_planes[0], w2_plane, w1_planes[1], w3_planes[1]):
+            nc.vector.memset(plane[:].bitcast(I32), 0)
+        nc.vector.memset(scattered[:], 0.0)
         make_identity(nc, identity[:])
 
         def load_pairs(c0, c1):
@@ -73,13 +74,13 @@ def tile_moe_res_glu_gelu_kernel(
             dst = pairs[:, 0 : 2 * T].rearrange("p (t e) -> p t e", e=2)
             nc.vector.tensor_copy(out=dst[:, c0:c1, :], in_=raw[:].rearrange("p e t -> p t e"))
 
-        def load_single(j, c0, c1):
+        def load_single(j, c0, c1, on_vector=0):
             raw = raw_pool.tile([P, c1 - c0], F32, name=f"raw{j}_{c0}")
             nc.sync.dma_start(out=raw[:], in_=x_rows[:, j, c0:c1])
-            if j == 2:
-                nc.vector.tensor_copy(out=singles[j][:, c0:c1], in_=raw[:])
-            else:
-                nc.scalar.copy(out=singles[j][:, c0:c1], in_=raw[:])
+            if on_vector > 0:
+                nc.vector.tensor_copy(out=singles[j][:, c0 : c0 + on_vector], in_=raw[:, 0:on_vector])
+            if on_vector < c1 - c0:
+                nc.scalar.copy(out=singles[j][:, c0 + on_vector : c1], in_=raw[:, on_vector : c1 - c0])
 
         def entries(s):
             return offsets[:, s * (SLICE // 16) : (s + 1) * (SLICE // 16)]
@@ -93,31 +94,32 @@ def tile_moe_res_glu_gelu_kernel(
         def gather_single(j, s):
             nc.scalar.activation(
                 grouped[s].rearrange("p (t d) -> p t d", d=4)[:, :, j],
-                singles[j][:, 0 : T + (16 if j == 3 and s >= 2 else 0)].indirect(entries(s)),
+                singles[j][:, 0 : T + (16 if j == 3 and s == 3 else 0)].indirect(entries(s)),
                 COPY,
             )
 
-        load_single(2, 0, 2048)
+        load_single(2, 0, 2048, 1408)
         nc.sync.dma_start(offsets[:], offs)
-        load_single(2, 2048, T)
+        load_single(2, 2048, T, 704)
         for s in range(slices):
             gather_single(2, s)
-        load_pairs(0, 1408)
-        load_pairs(1408, 2816)
-        load_pairs(2816, T)
+        load_pairs(0, 1280)
+        load_pairs(1280, 2304)
+        load_pairs(2304, 2816)
+        load_pairs(2816, 3072)
         for s in range(slices - 1):
             gather_pairs(s)
-        load_single(3, 0, 768)
-        load_single(3, 768, 1792)
-        load_single(3, 1792, 2688)
-        load_single(3, 2688, 3072)
+        load_single(3, 0, 512)
+        load_single(3, 512, 1280)
+        load_single(3, 1280, 2048)
+        load_single(3, 2048, 2816)
+        load_single(3, 2816, 3072)
 
         def load_scales(plane, scales, e0, e1):
-            wide = scales.shape[3]
             rows = scales[e0:e1].rearrange("e s (q r) i -> r q (e s) i", r=4)
             for r in range(4):
                 nc.sync.dma_start(
-                    out=plane[r:P:32, e0 * wide : e1 * wide].bitcast(I32).rearrange("q (e i) -> q e i", e=e1 - e0),
+                    out=plane[r:P:32, :].bitcast(I32).rearrange("q (e i) -> q e i", e=e1 - e0),
                     in_=rows[r].bitcast(I32),
                 )
 
@@ -128,17 +130,19 @@ def tile_moe_res_glu_gelu_kernel(
                 in_=words[e0:e1].rearrange("e s p b -> p (e s) b").bitcast(I32),
             )
 
-        load_scales(w1_plane, w1_scales, 0, E)
         load_words(w1_codes, w1_words, 0, 2)
-        load_scales(w3_plane, w3_scales, 0, E)
         load_words(w3_codes, w3_words, 0, 2)
-        load_words(w1_codes, w1_words, 2, 4)
-        load_words(w3_codes, w3_words, 2, 4)
+        load_scales(w1_planes[0], w1_scales, 0, RUN)
+        load_scales(w3_planes[0], w3_scales, 0, RUN)
+        load_words(w1_codes, w1_words, 2, 6)
+        load_words(w3_codes, w3_words, 2, 6)
         load_scales(w2_plane, w2_scales, 0, E)
         load_words(w2_codes, w2_words, 0, E)
         nc.sync.dma_start(out=gates[:, 0 : S // 2], in_=gate[:, 0 : S // 2])
-        load_words(w1_codes, w1_words, 4, E)
-        load_words(w3_codes, w3_words, 4, E)
+        load_scales(w1_planes[1], w1_scales, RUN, E)
+        load_scales(w3_planes[1], w3_scales, RUN, E)
+        load_words(w1_codes, w1_words, 6, E)
+        load_words(w3_codes, w3_words, 6, E)
         nc.sync.dma_start(out=gates[:, S // 2 : S], in_=gate[:, S // 2 : S])
         nc.sync.dma_start(out=residual[:], in_=xr)
 
@@ -156,14 +160,14 @@ def tile_moe_res_glu_gelu_kernel(
 
         def first_products(c):
             e, s, at = c // 2, c // 4, (c % 4) * P
-            for banks, codes, plane in ((a_banks, w1_codes, w1_plane), (b_banks, w3_codes, w3_plane)):
+            for banks, codes, planes in ((a_banks, w1_codes, w1_planes), (b_banks, w3_codes, w3_planes)):
                 banks[c] = psum.tile([P, H], F32, name="bank")
                 nc.tensor.matmul_mx(
                     out=banks[c][:],
                     lhsT=x_codes[s][:, at : at + P].bitcast(FP8X4),
                     lhsT_scale=x_scales[s][:, at : at + P],
                     rhs=codes[:, e * 2 * H : (e + 1) * 2 * H].bitcast(FP4X4),
-                    rhs_scale=plane[:, e * H : (e + 1) * H],
+                    rhs_scale=planes[e // RUN][:, (e % RUN) * H : (e % RUN + 1) * H],
                     start=True,
                     stop=True,
                 )
@@ -201,7 +205,8 @@ def tile_moe_res_glu_gelu_kernel(
                 h_grouped[e] = singles[3][:, T : T + 4 * C]
             else:
                 h_grouped[e] = work.tile([P, 4 * C], BF16, name="h_grouped", align_bytes=64)[:]
-            nc.scalar.copy(
+            copy = nc.vector.tensor_copy if e in () else nc.scalar.copy
+            copy(
                 out=h_grouped[e].bitcast(F32).rearrange("p (c r u) -> p c r u", c=2, u=2),
                 in_=turned[e][:].rearrange("p (c u r) -> p c r u", c=2, u=2),
             )
@@ -260,6 +265,8 @@ def tile_moe_res_glu_gelu_kernel(
         gather_pairs(3)
         gather_single(3, 1)
         quantise_tokens(1, 0, SLICE)
+        gather_single(3, 2)
+        quantise_tokens(2, 0, SLICE)
         chunks = S // P
         for c in range(3):
             first_products(c)
@@ -271,7 +278,7 @@ def tile_moe_res_glu_gelu_kernel(
             if c % 2 == 1 and c >= 3:
                 second_layer((c - 3) // 2)
             if c - 3 in (2 * e for e in LATE_AFTER):
-                late = 2 + LATE_AFTER.index((c - 3) // 2)
+                late = 3
                 gather_single(3, late)
                 quantise_tokens(late, 0, SLICE)
             if c + 3 < chunks:

@@ -57,7 +57,6 @@ def tile_moe_res_glu_gelu_kernel(
         w2_plane = keep.tile([P, E * N], U8, name="w2_plane", align_bytes=64)
         gates = keep.tile([P, S], F32, name="gates")
         residual = keep.tile([P, T], F32, name="residual")
-        scattered = keep.tile([P, T], F32, name="scattered")
         identity = keep.tile([P, P], F32, name="identity")
         warm = keep.tile([P, 1], F32, name="warm")
 
@@ -65,8 +64,9 @@ def tile_moe_res_glu_gelu_kernel(
         nc.scalar.activation(warm[:], warm[:], GELU)
         for plane in (w1_planes[0], w3_planes[0], w2_plane, w1_planes[1], w3_planes[1]):
             nc.vector.memset(plane[:].bitcast(I32), 0)
-        nc.vector.memset(scattered[:], 0.0)
         make_identity(nc, identity[:])
+
+        row2 = raw_pool.tile([P, T], F32, name="row2", tag="wide")
 
         def load_pairs(c0, c1):
             raw = raw_pool.tile([P, 2, c1 - c0], F32, name=f"raw_pairs{c0}")
@@ -75,8 +75,8 @@ def tile_moe_res_glu_gelu_kernel(
             nc.vector.tensor_copy(out=dst[:, c0:c1, :], in_=raw[:].rearrange("p e t -> p t e"))
 
         def load_single(j, c0, c1, on_vector=0):
-            raw = raw_pool.tile([P, c1 - c0], F32, name=f"raw{j}_{c0}")
-            nc.sync.dma_start(out=raw[:], in_=x_rows[:, j, c0:c1])
+            raw = row2[:, c0:c1] if j == 2 else raw_pool.tile([P, c1 - c0], F32, name=f"raw{j}_{c0}")[:]
+            nc.sync.dma_start(out=raw, in_=x_rows[:, j, c0:c1])
             if on_vector > 0:
                 nc.vector.tensor_copy(out=singles[j][:, c0 : c0 + on_vector], in_=raw[:, 0:on_vector])
             if on_vector < c1 - c0:
@@ -101,6 +101,8 @@ def tile_moe_res_glu_gelu_kernel(
         load_single(2, 0, 2048, 1408)
         nc.sync.dma_start(offsets[:], offs)
         load_single(2, 2048, T, 704)
+        scattered = raw_pool.tile([P, T], F32, name="scattered", tag="wide")
+        nc.vector.memset(scattered[:], 0.0)
         for s in range(slices):
             gather_single(2, s)
         load_pairs(0, 1280)

@@ -57,22 +57,29 @@ def tile_moe_res_glu_gelu_kernel(
         w2_plane = keep.tile([P, E * N], U8, name="w2_plane", align_bytes=64)
         gates = keep.tile([P, S], F32, name="gates")
         residual = keep.tile([P, T], F32, name="residual")
+        scattered = keep.tile([P, T], F32, name="scattered")
         identity = keep.tile([P, P], F32, name="identity")
         warm = keep.tile([P, 1], F32, name="warm")
 
         nc.vector.memset(warm[:], 0.0)
         nc.scalar.activation(warm[:], warm[:], GELU)
-        for plane in (w1_planes[0], w3_planes[0], w2_plane, w1_planes[1], w3_planes[1]):
+        for plane in (w1_planes[0], w3_planes[0], w2_plane):
             nc.vector.memset(plane[:].bitcast(I32), 0)
+        nc.vector.memset(scattered[:], 0.0)
+        for plane in (w1_planes[1], w3_planes[1]):
+            nc.gpsimd.memset(plane[:].bitcast(I32), 0)
         make_identity(nc, identity[:])
 
-        row2 = raw_pool.tile([P, T], F32, name="row2", tag="wide")
+        row2 = raw_pool.tile([P, T], F32, name="row2")
 
-        def load_pairs(c0, c1):
+        def load_pairs(c0, c1, on_scalar=0):
             raw = raw_pool.tile([P, 2, c1 - c0], F32, name=f"raw_pairs{c0}")
             nc.sync.dma_start(out=raw[:], in_=x_rows[:, 0:2, c0:c1])
             dst = pairs[:, 0 : 2 * T].rearrange("p (t e) -> p t e", e=2)
-            nc.vector.tensor_copy(out=dst[:, c0:c1, :], in_=raw[:].rearrange("p e t -> p t e"))
+            source = raw[:].rearrange("p e t -> p t e")
+            if on_scalar > 0:
+                nc.scalar.copy(out=dst[:, c0 : c0 + on_scalar, :], in_=source[:, 0:on_scalar, :])
+            nc.vector.tensor_copy(out=dst[:, c0 + on_scalar : c1, :], in_=source[:, on_scalar : c1 - c0, :])
 
         def load_single(j, c0, c1, on_vector=0):
             raw = row2[:, c0:c1] if j == 2 else raw_pool.tile([P, c1 - c0], F32, name=f"raw{j}_{c0}")[:]
@@ -101,21 +108,20 @@ def tile_moe_res_glu_gelu_kernel(
         load_single(2, 0, 2048, 1408)
         nc.sync.dma_start(offsets[:], offs)
         load_single(2, 2048, T, 704)
-        scattered = raw_pool.tile([P, T], F32, name="scattered", tag="wide")
-        nc.vector.memset(scattered[:], 0.0)
-        for s in range(slices):
+        nc.vector.tensor_copy(
+            grouped[3].rearrange("p (t d) -> p t d", d=4)[:, :, 2], row2[:].indirect(entries(3))
+        )
+        for s in range(slices - 1):
             gather_single(2, s)
-        load_pairs(0, 1280)
-        load_pairs(1280, 2304)
-        load_pairs(2304, 2816)
-        load_pairs(2816, 3072)
+        load_pairs(0, 1536)
+        load_pairs(1536, 2560)
+        load_pairs(2560, T, 160)
         for s in range(slices - 1):
             gather_pairs(s)
-        load_single(3, 0, 512)
-        load_single(3, 512, 1280)
-        load_single(3, 1280, 2048)
-        load_single(3, 2048, 2816)
-        load_single(3, 2816, 3072)
+        load_single(3, 0, 768)
+        load_single(3, 768, 1536)
+        load_single(3, 1536, 2304)
+        load_single(3, 2304, 3072)
 
         def load_scales(plane, scales, e0, e1):
             rows = scales[e0:e1].rearrange("e s (q r) i -> r q (e s) i", r=4)

@@ -20,9 +20,11 @@ P = 128
 K, T, E, C, H, N = 512, 3072, 8, 256, 512, 128
 S = E * C
 SLICE = 512
-CUTS = (0, 4, 7, 10, 13, 16)
-HELD_BY = (4, 10, 14)
-LATE_AFTER = (3,)
+CUTS = (0, 3, 6, 10, 13, 16)
+HELD_BY = {}
+UNITS = ((0, 1), (2,), (3,), (4, 5), (6, 7), (8, 9), (10, 11), (12, 13), (14, 15))
+ON_GPSIMD = ()
+LATE_AFTER = {4: 3}
 RUN = 4
 FLOPS = 2 * S * (2 * K * H + H * N)
 
@@ -37,14 +39,11 @@ def tile_moe_res_glu_gelu_kernel(
     with ExitStack() as ctx:
         keep = ctx.enter_context(tc.tile_pool(name="keep", bufs=1))
         raw_pool = ctx.enter_context(tc.tile_pool(name="raw", bufs=1))
-        slot_pool = ctx.enter_context(tc.tile_pool(name="slots", bufs=4))
-        work = ctx.enter_context(tc.tile_pool(name="work", bufs=4))
-        act_pool = ctx.enter_context(tc.tile_pool(name="acts", bufs=6))
-        psum = ctx.enter_context(tc.psum_pool(name="psum", bufs=8))
+        psum = ctx.enter_context(tc.psum_pool(name="psum", bufs=1))
 
         offsets = keep.tile([P, S // 16], U16, name="offsets")
         pairs = keep.tile([P, 2 * T + 4 * SLICE], BF16, name="pairs", align_bytes=64)
-        singles = {j: keep.tile([P, T + (j - 2) * 2 * H], BF16, name=f"single{j}", align_bytes=64) for j in (2, 3)}
+        singles = {j: keep.tile([P, T + (j - 2) * 4 * H], BF16, name=f"single{j}", align_bytes=64) for j in (2, 3)}
         grouped = [pairs[:, 2 * T : 2 * T + 4 * SLICE]]
         grouped.extend(
             keep.tile([P, 4 * SLICE], BF16, name=f"grouped{s}", align_bytes=64)[:] for s in range(1, slices)
@@ -98,10 +97,17 @@ def tile_moe_res_glu_gelu_kernel(
                 pairs[:].bitcast(U32)[:, 0 : T + (s // 3) * 2 * SLICE].indirect(entries(s)),
             )
 
+        behind, run_on = {}, {s: 0 for s in range(slices)}
+        reach = 0
+        for u in sorted(LATE_AFTER):
+            behind[u] = reach
+            run_on[LATE_AFTER[u]] = reach + 16
+            reach = reach + 4 * P * len(UNITS[u])
+
         def gather_single(j, s):
             nc.scalar.activation(
                 grouped[s].rearrange("p (t d) -> p t d", d=4)[:, :, j],
-                singles[j][:, 0 : T + (16 if j == 3 and s == 3 else 0)].indirect(entries(s)),
+                singles[j][:, 0 : T + (run_on[s] if j == 3 else 0)].indirect(entries(s)),
                 COPY,
             )
 
@@ -140,24 +146,29 @@ def tile_moe_res_glu_gelu_kernel(
 
         load_words(w1_codes, w1_words, 0, 2)
         load_words(w3_codes, w3_words, 0, 2)
-        load_scales(w1_planes[0], w1_scales, 0, RUN)
-        load_scales(w3_planes[0], w3_scales, 0, RUN)
-        load_words(w1_codes, w1_words, 2, 6)
-        load_words(w3_codes, w3_words, 2, 6)
+        load_scales(w1_planes[0], w1_scales, 0 * RUN, (0 + 1) * RUN)
+        load_scales(w3_planes[0], w3_scales, 0 * RUN, (0 + 1) * RUN)
+        load_words(w1_codes, w1_words, 2, 4)
+        load_words(w3_codes, w3_words, 2, 4)
         load_scales(w2_plane, w2_scales, 0, E)
-        load_words(w2_codes, w2_words, 0, E)
-        nc.sync.dma_start(out=gates[:, 0 : S // 2], in_=gate[:, 0 : S // 2])
-        load_scales(w1_planes[1], w1_scales, RUN, E)
-        load_scales(w3_planes[1], w3_scales, RUN, E)
-        load_words(w1_codes, w1_words, 6, E)
-        load_words(w3_codes, w3_words, 6, E)
-        nc.sync.dma_start(out=gates[:, S // 2 : S], in_=gate[:, S // 2 : S])
+        load_words(w2_codes, w2_words, 0, 4)
+        nc.sync.dma_start(out=gates[:, 0 * C : 2 * C], in_=gate[:, 0 * C : 2 * C])
+        load_scales(w1_planes[1], w1_scales, 1 * RUN, (1 + 1) * RUN)
+        load_scales(w3_planes[1], w3_scales, 1 * RUN, (1 + 1) * RUN)
+        load_words(w1_codes, w1_words, 4, 6)
+        load_words(w3_codes, w3_words, 4, 6)
+        load_words(w1_codes, w1_words, 6, 8)
+        load_words(w3_codes, w3_words, 6, 8)
+        load_words(w2_codes, w2_words, 4, 8)
+        nc.sync.dma_start(out=gates[:, 2 * C : 8 * C], in_=gate[:, 2 * C : 8 * C])
         nc.sync.dma_start(out=residual[:], in_=xr)
 
-        x_codes = [slot_pool.tile([P, SLICE], U32, name="x_codes", align_bytes=64) for s in range(slices)]
-        x_scales = [slot_pool.tile([P, SLICE], U8, name="x_scales", align_bytes=64) for s in range(slices)]
-        a_banks, b_banks, acts, hiddens, turned, h_grouped, h_codes, h_scales, y_banks = ({} for i in range(9))
+        x_codes = [keep.tile([P, SLICE], U32, name=f"x_codes{s}", align_bytes=64) for s in range(slices)]
+        x_scales = [keep.tile([P, SLICE], U8, name=f"x_scales{s}", align_bytes=64) for s in range(slices)]
+        a_banks, b_banks, acts, hiddens, turned, h_grouped, h_codes, h_scales, y_banks, ups = ({} for i in range(10))
         results = [keep.tile([P, H], F32, name=f"results{k}") for k in range(len(CUTS) - 1)]
+
+        taken = []
 
         def quantise_tokens(s, first, last):
             nc.vector.quantize_mx(
@@ -169,7 +180,7 @@ def tile_moe_res_glu_gelu_kernel(
         def first_products(c):
             e, s, at = c // 2, c // 4, (c % 4) * P
             for banks, codes, planes in ((a_banks, w1_codes, w1_planes), (b_banks, w3_codes, w3_planes)):
-                banks[c] = psum.tile([P, H], F32, name="bank")
+                banks[c] = bank() if banks is a_banks else psum.tile([P, H], F32, name=f"up{c % 4}")
                 nc.tensor.matmul_mx(
                     out=banks[c][:],
                     lhsT=x_codes[s][:, at : at + P].bitcast(FP8X4),
@@ -182,61 +193,75 @@ def tile_moe_res_glu_gelu_kernel(
 
         def activate(c):
             if c in HELD_BY:
-                acts[c] = results[HELD_BY.index(c)][:]
+                acts[c] = results[HELD_BY[c]][:]
             else:
-                acts[c] = act_pool.tile([P, H], F32, name="act")[:]
+                acts[c] = keep.tile([P, H], F32, name=f"act{c % 8}")[:]
             nc.scalar.activation(
                 acts[c].rearrange("s (u p e) -> s u p e", u=2, e=2),
                 a_banks[c][:].rearrange("s (p u e) -> s u p e", u=2, e=2),
                 GELU,
             )
+            if c in ON_GPSIMD:
+                ups[c] = keep.tile([P, H], F32, name=f"ups{c % 2}")
+                nc.scalar.copy(
+                    out=ups[c][:].rearrange("s (u p e) -> s u p e", u=2, e=2),
+                    in_=b_banks[c][:].rearrange("s (p u e) -> s u p e", u=2, e=2),
+                )
 
         def multiply(c):
-            hiddens[c] = work.tile([P, H], BF16, name="hidden", align_bytes=64)
-            nc.vector.tensor_tensor(
-                hiddens[c][:].rearrange("s (u p e) -> s u p e", u=2, e=2),
-                b_banks[c][:].rearrange("s (p u e) -> s u p e", u=2, e=2),
-                acts[c].rearrange("s (u p e) -> s u p e", u=2, e=2),
-                MULT,
-            )
-
-        def turn(c):
-            if c % 2 == 0:
-                turned[c // 2] = psum.tile([P, 4 * P], F32, name="bank")
-            words = hiddens[c][:].bitcast(F32)
-            for u in range(2):
-                place = (2 * (c % 2) + u) * P
-                nc.tensor.transpose(turned[c // 2][:, place : place + P], words[:, u * P : (u + 1) * P], identity[:])
-
-        def group_hidden(e):
-            if e in LATE_AFTER:
-                h_grouped[e] = singles[3][:, T : T + 4 * C]
+            hiddens[c] = keep.tile([P, H], BF16, name=f"hidden{c % 8}", align_bytes=64)
+            if c in ON_GPSIMD:
+                nc.gpsimd.tensor_tensor(hiddens[c][:], ups[c][:], acts[c], MULT)
             else:
-                h_grouped[e] = work.tile([P, 4 * C], BF16, name="h_grouped", align_bytes=64)[:]
-            copy = nc.vector.tensor_copy if e in () else nc.scalar.copy
-            copy(
-                out=h_grouped[e].bitcast(F32).rearrange("p (c r u) -> p c r u", c=2, u=2),
-                in_=turned[e][:].rearrange("p (c u r) -> p c r u", c=2, u=2),
+                nc.vector.tensor_tensor(
+                    hiddens[c][:].rearrange("s (u p e) -> s u p e", u=2, e=2),
+                    b_banks[c][:].rearrange("s (p u e) -> s u p e", u=2, e=2),
+                    acts[c].rearrange("s (u p e) -> s u p e", u=2, e=2),
+                    MULT,
+                )
+
+        def bank():
+            taken.append(len(taken))
+            return psum.tile([P, H], F32, name=f"short{taken[-1] % 4}")
+
+        def turn(u):
+            turned[u] = bank()
+            for n, c in enumerate(UNITS[u]):
+                words = hiddens[c][:].bitcast(F32)
+                for v in range(2):
+                    place = (2 * n + v) * P
+                    nc.tensor.transpose(turned[u][:, place : place + P], words[:, v * P : (v + 1) * P], identity[:])
+
+        def group_hidden(u):
+            count = len(UNITS[u])
+            if u in LATE_AFTER:
+                h_grouped[u] = singles[3][:, T + behind[u] : T + behind[u] + 4 * P * count]
+            else:
+                h_grouped[u] = keep.tile([P, 4 * P * count], BF16, name=f"h_grouped{u}", align_bytes=64)[:]
+            nc.scalar.copy(
+                out=h_grouped[u].bitcast(F32).rearrange("p (c r u) -> p c r u", c=count, u=2),
+                in_=turned[u][:, 0 : 2 * P * count].rearrange("p (c u r) -> p c r u", c=count, u=2),
             )
 
-        def quantise_hidden(e):
-            h_codes[e] = work.tile([P, C], U32, name="h_codes", align_bytes=64)
-            h_scales[e] = work.tile([P, C], U8, name="h_scales", align_bytes=64)
-            nc.vector.quantize_mx(out=h_codes[e][:].bitcast(FP8X4), scales=h_scales[e][:], in_=h_grouped[e])
+        def quantise_hidden(u):
+            width = P * len(UNITS[u])
+            h_codes[u] = keep.tile([P, width], U32, name=f"h_codes{u}", align_bytes=64)
+            h_scales[u] = keep.tile([P, width], U8, name=f"h_scales{u}", align_bytes=64)
+            nc.vector.quantize_mx(out=h_codes[u][:].bitcast(FP8X4), scales=h_scales[u][:], in_=h_grouped[u])
 
-        def second_product(e):
-            for k in range(len(CUTS) - 1):
-                first, last = max(CUTS[k], 2 * e), min(CUTS[k + 1], 2 * e + 2)
+        def second_products(k):
+            y_banks[k] = bank()
+            for u, unit in enumerate(UNITS):
+                first, last = max(CUTS[k], unit[0]), min(CUTS[k + 1], unit[-1] + 1)
                 if first < last:
-                    if first == CUTS[k]:
-                        y_banks[k] = psum.tile([P, SLICE], F32, name="bank")
-                    mine = slice((first - 2 * e) * P, (last - 2 * e) * P)
+                    e = first // 2
+                    mine = slice((first - unit[0]) * P, (last - unit[0]) * P)
                     nc.tensor.matmul_mx(
                         out=y_banks[k][:, (first - CUTS[k]) * P : (last - CUTS[k]) * P],
                         lhsT=w2_codes[:, e * 2 * N : (e + 1) * 2 * N].bitcast(FP4X4),
                         lhsT_scale=w2_plane[:, e * N : (e + 1) * N],
-                        rhs=h_codes[e][:, mine].bitcast(FP8X4),
-                        rhs_scale=h_scales[e][:, mine],
+                        rhs=h_codes[u][:, mine].bitcast(FP8X4),
+                        rhs_scale=h_scales[u][:, mine],
                         start=True,
                         stop=True,
                     )
@@ -254,19 +279,6 @@ def tile_moe_res_glu_gelu_kernel(
                 MULT,
             )
 
-        def gate_chunk(c):
-            activate(c)
-            multiply(c)
-
-        def turn_expert(e):
-            turn(2 * e)
-            turn(2 * e + 1)
-
-        def second_layer(e):
-            group_hidden(e)
-            quantise_hidden(e)
-            second_product(e)
-
         gather_single(3, 0)
         quantise_tokens(0, 0, C)
         quantise_tokens(0, C, SLICE)
@@ -275,28 +287,98 @@ def tile_moe_res_glu_gelu_kernel(
         quantise_tokens(1, 0, SLICE)
         gather_single(3, 2)
         quantise_tokens(2, 0, SLICE)
-        chunks = S // P
-        for c in range(3):
-            first_products(c)
-        for c in range(chunks + 2):
-            if c < chunks:
-                gate_chunk(c)
-            if c % 2 == 1 and c < chunks:
-                turn_expert(c // 2)
-            if c % 2 == 1 and c >= 3:
-                second_layer((c - 3) // 2)
-            if c - 3 in (2 * e for e in LATE_AFTER):
-                late = 3
-                gather_single(3, late)
-                quantise_tokens(late, 0, SLICE)
-            if c + 3 < chunks:
-                first_products(c + 3)
-            if c - 1 in HELD_BY:
-                collect(HELD_BY.index(c - 1))
-                scatter(HELD_BY.index(c - 1))
-        for k in range(len(HELD_BY), len(CUTS) - 1):
-            collect(k)
-            scatter(k)
+        first_products(0)
+        first_products(1)
+        first_products(2)
+        first_products(3)
+        activate(0)
+        multiply(0)
+        first_products(4)
+        activate(1)
+        multiply(1)
+        first_products(5)
+        activate(2)
+        multiply(2)
+        turn(0)
+        activate(3)
+        multiply(3)
+        turn(1)
+        activate(4)
+        multiply(4)
+        first_products(6)
+        activate(5)
+        multiply(5)
+        first_products(7)
+        group_hidden(0)
+        group_hidden(1)
+        quantise_hidden(0)
+        quantise_hidden(1)
+        second_products(0)
+        turn(2)
+        activate(6)
+        multiply(6)
+        turn(3)
+        activate(7)
+        multiply(7)
+        collect(0)
+        scatter(0)
+        turn(4)
+        group_hidden(2)
+        quantise_hidden(2)
+        group_hidden(3)
+        quantise_hidden(3)
+        group_hidden(4)
+        quantise_hidden(4)
+        gather_single(3, 3)
+        quantise_tokens(3, 0, SLICE)
+        first_products(8)
+        first_products(9)
+        first_products(10)
+        first_products(11)
+        activate(8)
+        multiply(8)
+        activate(9)
+        multiply(9)
+        first_products(12)
+        turn(5)
+        activate(10)
+        multiply(10)
+        second_products(1)
+        activate(11)
+        multiply(11)
+        first_products(13)
+        collect(1)
+        scatter(1)
+        turn(6)
+        group_hidden(5)
+        quantise_hidden(5)
+        activate(12)
+        multiply(12)
+        first_products(14)
+        first_products(15)
+        activate(13)
+        multiply(13)
+        group_hidden(6)
+        quantise_hidden(6)
+        turn(7)
+        activate(14)
+        multiply(14)
+        second_products(2)
+        activate(15)
+        multiply(15)
+        turn(8)
+        group_hidden(7)
+        collect(2)
+        quantise_hidden(7)
+        scatter(2)
+        group_hidden(8)
+        quantise_hidden(8)
+        second_products(3)
+        collect(3)
+        scatter(3)
+        second_products(4)
+        collect(4)
+        scatter(4)
 
         bounds = [0, 640, 1280, 1920, 2560, T]
         for c0, c1 in zip(bounds[:-1], bounds[1:]):

@@ -20,12 +20,19 @@ P = 128
 K, T, E, C, H, N = 512, 3072, 8, 256, 512, 128
 S = E * C
 SLICE = 512
+SLICES = S // SLICE
+CHUNKS = S // P
+LAST = SLICES - 1
 CUTS = (0, 3, 6, 10, 13, 16)
-HELD_BY = {}
-UNITS = ((0, 1), (2,), (3,), (4, 5), (6, 7), (8, 9), (10, 11), (12, 13), (14, 15))
-ON_GPSIMD = ()
-LATE_AFTER = {4: 3}
+UNIT_STARTS = sorted(set(range(0, CHUNKS, 2)) | set(CUTS))
+UNITS = [list(range(first, last)) for first, last in zip(UNIT_STARTS[:-1], UNIT_STARTS[1:])]
+GROUP_LAG = 3
+COLLECT_AFTER = (6, 12, 15)
+RING = 4
+TURN = 8
 RUN = 4
+RUN_ON = 16
+STORE = 640
 FLOPS = 2 * S * (2 * K * H + H * N)
 
 
@@ -33,8 +40,7 @@ def tile_moe_res_glu_gelu_kernel(
     tc, xT, xr, w1_words, w1_scales, w3_words, w3_scales, w2_words, w2_scales, gate, offs, out
 ):
     nc = tc.nc
-    x_rows = xT.rearrange("(p j) t -> p j t", j=4)
-    slices = S // SLICE
+    x_rows = xT.rearrange("(p d) t -> p d t", d=4)
 
     with ExitStack() as ctx:
         keep = ctx.enter_context(tc.tile_pool(name="keep", bufs=1))
@@ -43,10 +49,14 @@ def tile_moe_res_glu_gelu_kernel(
 
         offsets = keep.tile([P, S // 16], U16, name="offsets")
         pairs = keep.tile([P, 2 * T + 4 * SLICE], BF16, name="pairs", align_bytes=64)
-        singles = {j: keep.tile([P, T + (j - 2) * 4 * H], BF16, name=f"single{j}", align_bytes=64) for j in (2, 3)}
+        singles = {
+            2: keep.tile([P, T], BF16, name="single2", align_bytes=64),
+            3: keep.tile([P, T + 4 * P], BF16, name="single3", align_bytes=64),
+        }
+        behind_row3 = UNIT_STARTS.index(CUTS[1])
         grouped = [pairs[:, 2 * T : 2 * T + 4 * SLICE]]
         grouped.extend(
-            keep.tile([P, 4 * SLICE], BF16, name=f"grouped{s}", align_bytes=64)[:] for s in range(1, slices)
+            keep.tile([P, 4 * SLICE], BF16, name=f"grouped{s}", align_bytes=64)[:] for s in range(1, SLICES)
         )
         w1_codes = keep.tile([P, E * 2 * H], U8, name="w1_codes", align_bytes=64)
         w3_codes = keep.tile([P, E * 2 * H], U8, name="w3_codes", align_bytes=64)
@@ -71,71 +81,67 @@ def tile_moe_res_glu_gelu_kernel(
 
         row2 = raw_pool.tile([P, T], F32, name="row2")
 
-        def load_pairs(c0, c1, on_scalar=0):
+        def load_row2(c0, c1):
+            cut = c0 + (c1 - c0) * 11 // 16
+            nc.sync.dma_start(out=row2[:, c0:c1], in_=x_rows[:, 2, c0:c1])
+            nc.vector.tensor_copy(out=singles[2][:, c0:cut], in_=row2[:, c0:cut])
+            nc.scalar.copy(out=singles[2][:, cut:c1], in_=row2[:, cut:c1])
+
+        def load_pairs(c0, c1, on_scalar):
             raw = raw_pool.tile([P, 2, c1 - c0], F32, name=f"raw_pairs{c0}")
             nc.sync.dma_start(out=raw[:], in_=x_rows[:, 0:2, c0:c1])
-            dst = pairs[:, 0 : 2 * T].rearrange("p (t e) -> p t e", e=2)
-            source = raw[:].rearrange("p e t -> p t e")
+            table = pairs[:, 0 : 2 * T].rearrange("p (t d) -> p t d", d=2)
+            source = raw[:].rearrange("p d t -> p t d")
             if on_scalar > 0:
-                nc.scalar.copy(out=dst[:, c0 : c0 + on_scalar, :], in_=source[:, 0:on_scalar, :])
-            nc.vector.tensor_copy(out=dst[:, c0 + on_scalar : c1, :], in_=source[:, on_scalar : c1 - c0, :])
+                nc.scalar.copy(out=table[:, c0 : c0 + on_scalar, :], in_=source[:, 0:on_scalar, :])
+            nc.vector.tensor_copy(out=table[:, c0 + on_scalar : c1, :], in_=source[:, on_scalar : c1 - c0, :])
 
-        def load_single(j, c0, c1, on_vector=0):
-            raw = row2[:, c0:c1] if j == 2 else raw_pool.tile([P, c1 - c0], F32, name=f"raw{j}_{c0}")[:]
-            nc.sync.dma_start(out=raw, in_=x_rows[:, j, c0:c1])
-            if on_vector > 0:
-                nc.vector.tensor_copy(out=singles[j][:, c0 : c0 + on_vector], in_=raw[:, 0:on_vector])
-            if on_vector < c1 - c0:
-                nc.scalar.copy(out=singles[j][:, c0 + on_vector : c1], in_=raw[:, on_vector : c1 - c0])
+        def load_row3(c0, c1):
+            raw = raw_pool.tile([P, c1 - c0], F32, name=f"raw3_{c0}")
+            nc.sync.dma_start(out=raw[:], in_=x_rows[:, 3, c0:c1])
+            nc.scalar.copy(out=singles[3][:, c0:c1], in_=raw[:])
 
-        def entries(s):
-            return offsets[:, s * (SLICE // 16) : (s + 1) * (SLICE // 16)]
+        def entries(first, last):
+            return offsets[:, first // 16 : last // 16]
+
+        def of_slice(s):
+            return entries(s * SLICE, (s + 1) * SLICE)
+
+        def place_of_row(d, s):
+            return grouped[s].rearrange("p (t d) -> p t d", d=4)[:, :, d]
 
         def gather_pairs(s):
+            columns = T + 2 * SLICE if s == LAST else T
             nc.vector.tensor_copy(
                 grouped[s].bitcast(U32).rearrange("p (t u) -> p t u", u=2)[:, :, 0],
-                pairs[:].bitcast(U32)[:, 0 : T + (s // 3) * 2 * SLICE].indirect(entries(s)),
+                pairs[:].bitcast(U32)[:, 0:columns].indirect(of_slice(s)),
             )
 
-        behind, run_on = {}, {s: 0 for s in range(slices)}
-        reach = 0
-        for u in sorted(LATE_AFTER):
-            behind[u] = reach
-            run_on[LATE_AFTER[u]] = reach + 16
-            reach = reach + 4 * P * len(UNITS[u])
+        def gather_single(d, s):
+            columns = T + RUN_ON if (d, s) == (3, LAST) else T
+            nc.scalar.activation(place_of_row(d, s), singles[d][:, 0:columns].indirect(of_slice(s)), COPY)
 
-        def gather_single(j, s):
-            nc.scalar.activation(
-                grouped[s].rearrange("p (t d) -> p t d", d=4)[:, :, j],
-                singles[j][:, 0 : T + (run_on[s] if j == 3 else 0)].indirect(entries(s)),
-                COPY,
-            )
-
-        load_single(2, 0, 2048, 1408)
+        load_row2(0, 2048)
         nc.sync.dma_start(offsets[:], offs)
-        load_single(2, 2048, T, 704)
-        nc.vector.tensor_copy(
-            grouped[3].rearrange("p (t d) -> p t d", d=4)[:, :, 2], row2[:].indirect(entries(3))
-        )
-        for s in range(slices - 1):
+        load_row2(2048, T)
+        nc.vector.tensor_copy(place_of_row(2, LAST), row2[:].indirect(of_slice(LAST)))
+        for s in range(LAST):
             gather_single(2, s)
-        load_pairs(0, 1536)
-        load_pairs(1536, 2560)
-        load_pairs(2560, T, 160)
-        for s in range(slices - 1):
+        load_pairs(0, 1536, 0)
+        load_pairs(1536, 2560, 0)
+        load_pairs(2560, T, (T - 2560) * 5 // 16)
+        for s in range(LAST):
             gather_pairs(s)
-        load_single(3, 0, 768)
-        load_single(3, 768, 1536)
-        load_single(3, 1536, 2304)
-        load_single(3, 2304, 3072)
+        for c0 in range(0, T, T // 4):
+            load_row3(c0, c0 + T // 4)
 
-        def load_scales(plane, scales, e0, e1):
-            rows = scales[e0:e1].rearrange("e s (q r) i -> r q (e s) i", r=4)
+        def load_scales(sources, e0, e1):
             for r in range(4):
-                nc.sync.dma_start(
-                    out=plane[r:P:32, :].bitcast(I32).rearrange("q (e i) -> q e i", e=e1 - e0),
-                    in_=rows[r].bitcast(I32),
-                )
+                for plane, scales in sources:
+                    nc.sync.dma_start(
+                        out=plane[r:P:32, :].bitcast(I32).rearrange("q (e i) -> q e i", e=e1 - e0),
+                        in_=scales[e0:e1].rearrange("e s (q r) i -> r q (e s) i", r=4)[r].bitcast(I32),
+                    )
 
         def load_words(codes, words, e0, e1):
             wide = words.shape[3]
@@ -144,31 +150,40 @@ def tile_moe_res_glu_gelu_kernel(
                 in_=words[e0:e1].rearrange("e s p b -> p (e s) b").bitcast(I32),
             )
 
-        load_words(w1_codes, w1_words, 0, 2)
-        load_words(w3_codes, w3_words, 0, 2)
-        load_scales(w1_planes[0], w1_scales, 0 * RUN, (0 + 1) * RUN)
-        load_scales(w3_planes[0], w3_scales, 0 * RUN, (0 + 1) * RUN)
-        load_words(w1_codes, w1_words, 2, 4)
-        load_words(w3_codes, w3_words, 2, 4)
-        load_scales(w2_plane, w2_scales, 0, E)
-        load_words(w2_codes, w2_words, 0, 4)
-        nc.sync.dma_start(out=gates[:, 0 * C : 2 * C], in_=gate[:, 0 * C : 2 * C])
-        load_scales(w1_planes[1], w1_scales, 1 * RUN, (1 + 1) * RUN)
-        load_scales(w3_planes[1], w3_scales, 1 * RUN, (1 + 1) * RUN)
-        load_words(w1_codes, w1_words, 4, 6)
-        load_words(w3_codes, w3_words, 4, 6)
-        load_words(w1_codes, w1_words, 6, 8)
-        load_words(w3_codes, w3_words, 6, 8)
-        load_words(w2_codes, w2_words, 4, 8)
-        nc.sync.dma_start(out=gates[:, 2 * C : 8 * C], in_=gate[:, 2 * C : 8 * C])
+        def load_first_words(s):
+            load_words(w1_codes, w1_words, 2 * s, 2 * s + 2)
+            load_words(w3_codes, w3_words, 2 * s, 2 * s + 2)
+
+        load_first_words(0)
+        load_scales(((w1_planes[0], w1_scales), (w3_planes[0], w3_scales)), 0, RUN)
+        load_first_words(1)
+        load_scales(((w2_plane, w2_scales),), 0, E)
+        load_words(w2_codes, w2_words, 0, RUN)
+        nc.sync.dma_start(out=gates[:, 0:SLICE], in_=gate[:, 0:SLICE])
+        load_scales(((w1_planes[1], w1_scales),), RUN, E)
+        load_scales(((w3_planes[1], w3_scales),), RUN, E)
+        load_first_words(2)
+        load_first_words(3)
+        load_words(w2_codes, w2_words, RUN, E)
+        nc.sync.dma_start(out=gates[:, SLICE:S], in_=gate[:, SLICE:S])
         nc.sync.dma_start(out=residual[:], in_=xr)
 
-        x_codes = [keep.tile([P, SLICE], U32, name=f"x_codes{s}", align_bytes=64) for s in range(slices)]
-        x_scales = [keep.tile([P, SLICE], U8, name=f"x_scales{s}", align_bytes=64) for s in range(slices)]
-        a_banks, b_banks, acts, hiddens, turned, h_grouped, h_codes, h_scales, y_banks, ups = ({} for i in range(10))
-        results = [keep.tile([P, H], F32, name=f"results{k}") for k in range(len(CUTS) - 1)]
+        x_codes = [keep.tile([P, SLICE], U32, name=f"x_codes{s}", align_bytes=64) for s in range(SLICES)]
+        x_scales = [keep.tile([P, SLICE], U8, name=f"x_scales{s}", align_bytes=64) for s in range(SLICES)]
+        results = [keep.tile([P, SLICE], F32, name=f"results{k}") for k in range(len(CUTS) - 1)]
+        a_banks, b_banks, hiddens, turned, h_codes, h_scales, y_banks = ({} for kind in range(7))
 
-        taken = []
+        steps = []
+        for c in range(CHUNKS):
+            steps.append(("gate", c))
+            steps.extend(("group", u) for u, unit in enumerate(UNITS) if unit[-1] + GROUP_LAG == c)
+            if c in COLLECT_AFTER:
+                steps.append(("collect", COLLECT_AFTER.index(c)))
+        steps.extend(("group", u) for u, unit in enumerate(UNITS) if unit[-1] + GROUP_LAG >= CHUNKS)
+        steps.extend(("collect", k) for k in range(len(COLLECT_AFTER), len(CUTS) - 1))
+
+        def bank_of(step):
+            return psum.tile([P, H], F32, name=f"step{steps.index(step) % RING}")
 
         def quantise_tokens(s, first, last):
             nc.vector.quantize_mx(
@@ -177,103 +192,82 @@ def tile_moe_res_glu_gelu_kernel(
                 in_=grouped[s][:, 4 * first : 4 * last],
             )
 
-        def first_products(c):
+        def first_product(bank, c, codes, planes):
             e, s, at = c // 2, c // 4, (c % 4) * P
-            for banks, codes, planes in ((a_banks, w1_codes, w1_planes), (b_banks, w3_codes, w3_planes)):
-                banks[c] = bank() if banks is a_banks else psum.tile([P, H], F32, name=f"up{c % 4}")
+            nc.tensor.matmul_mx(
+                out=bank[:],
+                lhsT=x_codes[s][:, at : at + P].bitcast(FP8X4),
+                lhsT_scale=x_scales[s][:, at : at + P],
+                rhs=codes[:, e * 2 * H : (e + 1) * 2 * H].bitcast(FP4X4),
+                rhs_scale=planes[e // RUN][:, (e % RUN) * H : (e % RUN + 1) * H],
+                start=True,
+                stop=True,
+            )
+
+        def first_products(c):
+            a_banks[c] = bank_of(("gate", c))
+            first_product(a_banks[c], c, w1_codes, w1_planes)
+            b_banks[c] = psum.tile([P, H], F32, name=f"up{c % RING}")
+            first_product(b_banks[c], c, w3_codes, w3_planes)
+
+        def from_bank(bank):
+            return bank[:].rearrange("s (p u e) -> s u p e", u=2, e=2)
+
+        def by_words(tile):
+            return tile[:].rearrange("s (u p e) -> s u p e", u=2, e=2)
+
+        def gate_chunk(c):
+            act = keep.tile([P, H], F32, name=f"act{c % TURN}")
+            nc.scalar.activation(by_words(act), from_bank(a_banks[c]), GELU)
+            hiddens[c] = keep.tile([P, H], BF16, name=f"hidden{c % TURN}", align_bytes=64)
+            nc.vector.tensor_tensor(by_words(hiddens[c]), from_bank(b_banks[c]), by_words(act), MULT)
+
+        def turn(u):
+            turned[u] = bank_of(("group", u))
+            for n, c in enumerate(UNITS[u]):
+                words = hiddens[c][:].bitcast(F32)
+                for half in range(2):
+                    place = (2 * n + half) * P
+                    nc.tensor.transpose(
+                        turned[u][:, place : place + P], words[:, half * P : (half + 1) * P], identity[:]
+                    )
+
+        def group_unit(u):
+            count = len(UNITS[u])
+            if u == behind_row3:
+                h_grouped = singles[3][:, T : T + 4 * P * count]
+            else:
+                h_grouped = keep.tile([P, 4 * P * count], BF16, name=f"h_grouped{u}", align_bytes=64)[:]
+            nc.scalar.copy(
+                out=h_grouped.bitcast(F32).rearrange("p (c s u) -> p c s u", c=count, u=2),
+                in_=turned[u][:, 0 : 2 * P * count].rearrange("p (c u s) -> p c s u", c=count, u=2),
+            )
+            h_codes[u] = keep.tile([P, P * count], U32, name=f"h_codes{u}", align_bytes=64)
+            h_scales[u] = keep.tile([P, P * count], U8, name=f"h_scales{u}", align_bytes=64)
+            nc.vector.quantize_mx(out=h_codes[u][:].bitcast(FP8X4), scales=h_scales[u][:], in_=h_grouped)
+
+        def units_of(k):
+            return [u for u, unit in enumerate(UNITS) if CUTS[k] <= unit[0] < CUTS[k + 1]]
+
+        def second_products(k):
+            y_banks[k] = bank_of(("collect", k))
+            for u in units_of(k):
+                e, at = UNITS[u][0] // 2, (UNITS[u][0] - CUTS[k]) * P
                 nc.tensor.matmul_mx(
-                    out=banks[c][:],
-                    lhsT=x_codes[s][:, at : at + P].bitcast(FP8X4),
-                    lhsT_scale=x_scales[s][:, at : at + P],
-                    rhs=codes[:, e * 2 * H : (e + 1) * 2 * H].bitcast(FP4X4),
-                    rhs_scale=planes[e // RUN][:, (e % RUN) * H : (e % RUN + 1) * H],
+                    out=y_banks[k][:, at : at + P * len(UNITS[u])],
+                    lhsT=w2_codes[:, e * 2 * N : (e + 1) * 2 * N].bitcast(FP4X4),
+                    lhsT_scale=w2_plane[:, e * N : (e + 1) * N],
+                    rhs=h_codes[u][:].bitcast(FP8X4),
+                    rhs_scale=h_scales[u][:],
                     start=True,
                     stop=True,
                 )
 
-        def activate(c):
-            if c in HELD_BY:
-                acts[c] = results[HELD_BY[c]][:]
-            else:
-                acts[c] = keep.tile([P, H], F32, name=f"act{c % 8}")[:]
-            nc.scalar.activation(
-                acts[c].rearrange("s (u p e) -> s u p e", u=2, e=2),
-                a_banks[c][:].rearrange("s (p u e) -> s u p e", u=2, e=2),
-                GELU,
-            )
-            if c in ON_GPSIMD:
-                ups[c] = keep.tile([P, H], F32, name=f"ups{c % 2}")
-                nc.scalar.copy(
-                    out=ups[c][:].rearrange("s (u p e) -> s u p e", u=2, e=2),
-                    in_=b_banks[c][:].rearrange("s (p u e) -> s u p e", u=2, e=2),
-                )
-
-        def multiply(c):
-            hiddens[c] = keep.tile([P, H], BF16, name=f"hidden{c % 8}", align_bytes=64)
-            if c in ON_GPSIMD:
-                nc.gpsimd.tensor_tensor(hiddens[c][:], ups[c][:], acts[c], MULT)
-            else:
-                nc.vector.tensor_tensor(
-                    hiddens[c][:].rearrange("s (u p e) -> s u p e", u=2, e=2),
-                    b_banks[c][:].rearrange("s (p u e) -> s u p e", u=2, e=2),
-                    acts[c].rearrange("s (u p e) -> s u p e", u=2, e=2),
-                    MULT,
-                )
-
-        def bank():
-            taken.append(len(taken))
-            return psum.tile([P, H], F32, name=f"short{taken[-1] % 4}")
-
-        def turn(u):
-            turned[u] = bank()
-            for n, c in enumerate(UNITS[u]):
-                words = hiddens[c][:].bitcast(F32)
-                for v in range(2):
-                    place = (2 * n + v) * P
-                    nc.tensor.transpose(turned[u][:, place : place + P], words[:, v * P : (v + 1) * P], identity[:])
-
-        def group_hidden(u):
-            count = len(UNITS[u])
-            if u in LATE_AFTER:
-                h_grouped[u] = singles[3][:, T + behind[u] : T + behind[u] + 4 * P * count]
-            else:
-                h_grouped[u] = keep.tile([P, 4 * P * count], BF16, name=f"h_grouped{u}", align_bytes=64)[:]
-            nc.scalar.copy(
-                out=h_grouped[u].bitcast(F32).rearrange("p (c r u) -> p c r u", c=count, u=2),
-                in_=turned[u][:, 0 : 2 * P * count].rearrange("p (c u r) -> p c r u", c=count, u=2),
-            )
-
-        def quantise_hidden(u):
-            width = P * len(UNITS[u])
-            h_codes[u] = keep.tile([P, width], U32, name=f"h_codes{u}", align_bytes=64)
-            h_scales[u] = keep.tile([P, width], U8, name=f"h_scales{u}", align_bytes=64)
-            nc.vector.quantize_mx(out=h_codes[u][:].bitcast(FP8X4), scales=h_scales[u][:], in_=h_grouped[u])
-
-        def second_products(k):
-            y_banks[k] = bank()
-            for u, unit in enumerate(UNITS):
-                first, last = max(CUTS[k], unit[0]), min(CUTS[k + 1], unit[-1] + 1)
-                if first < last:
-                    e = first // 2
-                    mine = slice((first - unit[0]) * P, (last - unit[0]) * P)
-                    nc.tensor.matmul_mx(
-                        out=y_banks[k][:, (first - CUTS[k]) * P : (last - CUTS[k]) * P],
-                        lhsT=w2_codes[:, e * 2 * N : (e + 1) * 2 * N].bitcast(FP4X4),
-                        lhsT_scale=w2_plane[:, e * N : (e + 1) * N],
-                        rhs=h_codes[u][:, mine].bitcast(FP8X4),
-                        rhs_scale=h_scales[u][:, mine],
-                        start=True,
-                        stop=True,
-                    )
-
-        def collect(k):
-            width = (CUTS[k + 1] - CUTS[k]) * P
-            nc.scalar.copy(out=results[k][:, 0:width], in_=y_banks[k][:, 0:width])
-
-        def scatter(k):
+        def put_back(k):
             first, last = CUTS[k] * P, CUTS[k + 1] * P
+            nc.scalar.copy(out=results[k][:, 0 : last - first], in_=y_banks[k][:, 0 : last - first])
             nc.vector.tensor_tensor(
-                scattered[:].indirect(offsets[:, first // 16 : last // 16]),
+                scattered[:].indirect(entries(first, last)),
                 results[k][:, 0 : last - first],
                 gates[:, first:last],
                 MULT,
@@ -282,105 +276,34 @@ def tile_moe_res_glu_gelu_kernel(
         gather_single(3, 0)
         quantise_tokens(0, 0, C)
         quantise_tokens(0, C, SLICE)
-        gather_pairs(3)
-        gather_single(3, 1)
-        quantise_tokens(1, 0, SLICE)
-        gather_single(3, 2)
-        quantise_tokens(2, 0, SLICE)
-        first_products(0)
-        first_products(1)
-        first_products(2)
-        first_products(3)
-        activate(0)
-        multiply(0)
-        first_products(4)
-        activate(1)
-        multiply(1)
-        first_products(5)
-        activate(2)
-        multiply(2)
-        turn(0)
-        activate(3)
-        multiply(3)
-        turn(1)
-        activate(4)
-        multiply(4)
-        first_products(6)
-        activate(5)
-        multiply(5)
-        first_products(7)
-        group_hidden(0)
-        group_hidden(1)
-        quantise_hidden(0)
-        quantise_hidden(1)
-        second_products(0)
-        turn(2)
-        activate(6)
-        multiply(6)
-        turn(3)
-        activate(7)
-        multiply(7)
-        collect(0)
-        scatter(0)
-        turn(4)
-        group_hidden(2)
-        quantise_hidden(2)
-        group_hidden(3)
-        quantise_hidden(3)
-        group_hidden(4)
-        quantise_hidden(4)
-        gather_single(3, 3)
-        quantise_tokens(3, 0, SLICE)
-        first_products(8)
-        first_products(9)
-        first_products(10)
-        first_products(11)
-        activate(8)
-        multiply(8)
-        activate(9)
-        multiply(9)
-        first_products(12)
-        turn(5)
-        activate(10)
-        multiply(10)
-        second_products(1)
-        activate(11)
-        multiply(11)
-        first_products(13)
-        collect(1)
-        scatter(1)
-        turn(6)
-        group_hidden(5)
-        quantise_hidden(5)
-        activate(12)
-        multiply(12)
-        first_products(14)
-        first_products(15)
-        activate(13)
-        multiply(13)
-        group_hidden(6)
-        quantise_hidden(6)
-        turn(7)
-        activate(14)
-        multiply(14)
-        second_products(2)
-        activate(15)
-        multiply(15)
-        turn(8)
-        group_hidden(7)
-        collect(2)
-        quantise_hidden(7)
-        scatter(2)
-        group_hidden(8)
-        quantise_hidden(8)
-        second_products(3)
-        collect(3)
-        scatter(3)
-        second_products(4)
-        collect(4)
-        scatter(4)
+        gather_pairs(LAST)
+        for s in range(1, LAST):
+            gather_single(3, s)
+            quantise_tokens(s, 0, SLICE)
 
-        bounds = [0, 640, 1280, 1920, 2560, T]
-        for c0, c1 in zip(bounds[:-1], bounds[1:]):
+        def input_step(step):
+            kind, n = step
+            if kind == "group":
+                return ("gate", UNITS[n][-1])
+            if kind == "collect":
+                return ("group", units_of(n)[-1])
+            return steps[0]
+
+        fill = {"gate": first_products, "group": turn, "collect": second_products}
+        empty = {"gate": gate_chunk, "group": group_unit, "collect": put_back}
+        for kind, n in steps[:RING]:
+            fill[kind](n)
+        filled = RING
+        for at, (kind, n) in enumerate(steps):
+            empty[kind](n)
+            if (kind, n) == ("collect", 0):
+                gather_single(3, LAST)
+                quantise_tokens(LAST, 0, SLICE)
+            while filled < len(steps) and filled <= at + RING and steps.index(input_step(steps[filled])) <= at:
+                fill[steps[filled][0]](steps[filled][1])
+                filled = filled + 1
+
+        for c0 in range(0, T, STORE):
+            c1 = min(c0 + STORE, T)
             nc.vector.tensor_tensor(residual[:, c0:c1], residual[:, c0:c1], scattered[:, c0:c1], ADD)
             nc.sync.dma_start(out=out[:, c0:c1], in_=residual[:, c0:c1])

@@ -28,6 +28,7 @@ UNIT_STARTS = sorted(set(range(0, CHUNKS, 2)) | set(CUTS))
 UNITS = [list(range(first, last)) for first, last in zip(UNIT_STARTS[:-1], UNIT_STARTS[1:])]
 GROUP_LAG = 3
 COLLECT_AFTER = (6, 12, 15)
+ON_GPSIMD = 14
 RING = 4
 TURN = 8
 RUN = 4
@@ -173,13 +174,17 @@ def tile_moe_res_glu_gelu_kernel(
         results = [keep.tile([P, SLICE], F32, name=f"results{k}") for k in range(len(CUTS) - 1)]
         a_banks, b_banks, hiddens, turned, h_codes, h_scales, y_banks = ({} for kind in range(7))
 
+        def due_after(unit):
+            c = unit[-1] + GROUP_LAG
+            return c if c < ON_GPSIMD else max(c, CHUNKS - 1)
+
         steps = []
         for c in range(CHUNKS):
             steps.append(("gate", c))
-            steps.extend(("group", u) for u, unit in enumerate(UNITS) if unit[-1] + GROUP_LAG == c)
+            steps.extend(("group", u) for u, unit in enumerate(UNITS) if due_after(unit) == c)
             if c in COLLECT_AFTER:
                 steps.append(("collect", COLLECT_AFTER.index(c)))
-        steps.extend(("group", u) for u, unit in enumerate(UNITS) if unit[-1] + GROUP_LAG >= CHUNKS)
+        steps.extend(("group", u) for u, unit in enumerate(UNITS) if due_after(unit) >= CHUNKS)
         steps.extend(("collect", k) for k in range(len(COLLECT_AFTER), len(CUTS) - 1))
 
         def bank_of(step):
@@ -220,7 +225,12 @@ def tile_moe_res_glu_gelu_kernel(
             act = keep.tile([P, H], F32, name=f"act{c % TURN}")
             nc.scalar.activation(by_words(act), from_bank(a_banks[c]), GELU)
             hiddens[c] = keep.tile([P, H], BF16, name=f"hidden{c % TURN}", align_bytes=64)
-            nc.vector.tensor_tensor(by_words(hiddens[c]), from_bank(b_banks[c]), by_words(act), MULT)
+            if c == ON_GPSIMD:
+                up = keep.tile([P, H], F32, name="up_copy")
+                nc.scalar.copy(out=by_words(up), in_=from_bank(b_banks[c]))
+                nc.gpsimd.tensor_tensor(hiddens[c][:], up[:], act[:], MULT)
+            else:
+                nc.vector.tensor_tensor(by_words(hiddens[c]), from_bank(b_banks[c]), by_words(act), MULT)
 
         def turn(u):
             turned[u] = bank_of(("group", u))

@@ -100,7 +100,10 @@ def tile_moe_res_glu_gelu_kernel(
         def load_row3(c0, c1):
             raw = raw_pool.tile([P, c1 - c0], F32, name=f"raw3_{c0}")
             nc.sync.dma_start(out=raw[:], in_=x_rows[:, 3, c0:c1])
-            nc.scalar.copy(out=singles[3][:, c0:c1], in_=raw[:])
+            cut = (c0 + c1) // 2 if c1 == T else c1
+            nc.scalar.copy(out=singles[3][:, c0:cut], in_=raw[:, 0 : cut - c0])
+            if cut < c1:
+                nc.gpsimd.tensor_copy(out=singles[3][:, cut:c1], in_=raw[:, cut - c0 : c1 - c0])
 
         def entries(first, last):
             return offsets[:, first // 16 : last // 16]

@@ -22,17 +22,18 @@ S = E * C
 SLICE = 512
 SLICES = S // SLICE
 CHUNKS = S // P
-LAST = SLICES - 1
 CUTS = (0, 3, 6, 10, 13, 16)
 UNIT_STARTS = sorted(set(range(0, CHUNKS, 2)) | set(CUTS))
 UNITS = [list(range(first, last)) for first, last in zip(UNIT_STARTS[:-1], UNIT_STARTS[1:])]
-GROUP_LAG = 3
-COLLECT_AFTER = (6, 12, 15)
-ON_GPSIMD = 14
+ON_GPSIMD = (10, 13)
+UPS = 3
+GROUP_AFTER = (5, 9, 12, 15, 16)
+COLLECT_AFTER = (9, 12, 15, 16, 17)
+LOADS = 0
+ON_VECTOR = (1024, 512, 768, 512)
 RING = 4
 TURN = 8
-RUN = 4
-RUN_ON = 16
+RUN = 8
 STORE = 640
 FLOPS = 2 * S * (2 * K * H + H * N)
 
@@ -49,16 +50,9 @@ def tile_moe_res_glu_gelu_kernel(
         psum = ctx.enter_context(tc.psum_pool(name="psum", bufs=1))
 
         offsets = keep.tile([P, S // 16], U16, name="offsets")
-        pairs = keep.tile([P, 2 * T + 4 * SLICE], BF16, name="pairs", align_bytes=64)
-        singles = {
-            2: keep.tile([P, T], BF16, name="single2", align_bytes=64),
-            3: keep.tile([P, T + 4 * P], BF16, name="single3", align_bytes=64),
-        }
-        behind_row3 = UNIT_STARTS.index(CUTS[1])
-        grouped = [pairs[:, 2 * T : 2 * T + 4 * SLICE]]
-        grouped.extend(
-            keep.tile([P, 4 * SLICE], BF16, name=f"grouped{s}", align_bytes=64)[:] for s in range(1, SLICES)
-        )
+        rows = [raw_pool.tile([P, T], F32, name=f"row{d}") for d in range(4)]
+        picked = [[keep.tile([P, 2, SLICE], BF16, name=f"picked{u}_{s}") for s in range(SLICES)] for u in range(2)]
+        grouped = [keep.tile([P, 4 * SLICE], BF16, name=f"grouped{s}", align_bytes=64) for s in range(SLICES)]
         w1_codes = keep.tile([P, E * 2 * H], U8, name="w1_codes", align_bytes=64)
         w3_codes = keep.tile([P, E * 2 * H], U8, name="w3_codes", align_bytes=64)
         w2_codes = keep.tile([P, E * 2 * N], U8, name="w2_codes", align_bytes=64)
@@ -73,71 +67,41 @@ def tile_moe_res_glu_gelu_kernel(
 
         nc.vector.memset(warm[:], 0.0)
         nc.scalar.activation(warm[:], warm[:], GELU)
-        for plane in (w1_planes[0], w3_planes[0], w2_plane):
+        for plane in w1_planes + w3_planes + [w2_plane]:
             nc.vector.memset(plane[:].bitcast(I32), 0)
         nc.vector.memset(scattered[:], 0.0)
-        for plane in (w1_planes[1], w3_planes[1]):
-            nc.gpsimd.memset(plane[:].bitcast(I32), 0)
         make_identity(nc, identity[:])
-
-        row2 = raw_pool.tile([P, T], F32, name="row2")
-
-        def load_row2(c0, c1):
-            cut = c0 + (c1 - c0) * 11 // 16
-            nc.sync.dma_start(out=row2[:, c0:c1], in_=x_rows[:, 2, c0:c1])
-            nc.vector.tensor_copy(out=singles[2][:, c0:cut], in_=row2[:, c0:cut])
-            nc.scalar.copy(out=singles[2][:, cut:c1], in_=row2[:, cut:c1])
-
-        def load_pairs(c0, c1, on_scalar):
-            raw = raw_pool.tile([P, 2, c1 - c0], F32, name=f"raw_pairs{c0}")
-            nc.sync.dma_start(out=raw[:], in_=x_rows[:, 0:2, c0:c1])
-            table = pairs[:, 0 : 2 * T].rearrange("p (t d) -> p t d", d=2)
-            source = raw[:].rearrange("p d t -> p t d")
-            if on_scalar > 0:
-                nc.scalar.copy(out=table[:, c0 : c0 + on_scalar, :], in_=source[:, 0:on_scalar, :])
-            nc.vector.tensor_copy(out=table[:, c0 + on_scalar : c1, :], in_=source[:, on_scalar : c1 - c0, :])
-
-        def load_row3(c0, c1):
-            raw = raw_pool.tile([P, c1 - c0], F32, name=f"raw3_{c0}")
-            nc.sync.dma_start(out=raw[:], in_=x_rows[:, 3, c0:c1])
-            cut = (c0 + c1) // 2 if c1 == T else c1
-            nc.scalar.copy(out=singles[3][:, c0:cut], in_=raw[:, 0 : cut - c0])
-            if cut < c1:
-                nc.gpsimd.tensor_copy(out=singles[3][:, cut:c1], in_=raw[:, cut - c0 : c1 - c0])
 
         def entries(first, last):
             return offsets[:, first // 16 : last // 16]
 
-        def of_slice(s):
-            return entries(s * SLICE, (s + 1) * SLICE)
+        def gather(d, first, last, on_vector):
+            s, at = first // SLICE, first % SLICE
+            target = picked[d // 2][s][:, d % 2, at : at + last - first]
+            if on_vector:
+                nc.vector.tensor_copy(target, rows[d][:].indirect(entries(first, last)))
+            else:
+                nc.scalar.activation(target, rows[d][:].indirect(entries(first, last)), COPY)
 
-        def place_of_row(d, s):
-            return grouped[s].rearrange("p (t d) -> p t d", d=4)[:, :, d]
+        def gather_row(d):
+            cuts = sorted(set(range(0, S + 1, SLICE)) | {ON_VECTOR[d]} | ({C} if d == 3 else set()))
+            for first, last in zip(cuts[:-1], cuts[1:]):
+                gather(d, first, last, last <= ON_VECTOR[d])
 
-        def gather_pairs(s):
-            columns = T + 2 * SLICE if s == LAST else T
+        def place(u, s, first, last):
             nc.vector.tensor_copy(
-                grouped[s].bitcast(U32).rearrange("p (t u) -> p t u", u=2)[:, :, 0],
-                pairs[:].bitcast(U32)[:, 0:columns].indirect(of_slice(s)),
+                out=grouped[s][:].rearrange("p (t d) -> p t d", d=4)[:, first:last, 2 * u : 2 * u + 2],
+                in_=picked[u][s][:].rearrange("p d t -> p t d")[:, first:last, :],
             )
 
-        def gather_single(d, s):
-            columns = T + RUN_ON if (d, s) == (3, LAST) else T
-            nc.scalar.activation(place_of_row(d, s), singles[d][:, 0:columns].indirect(of_slice(s)), COPY)
-
-        load_row2(0, 2048)
-        nc.sync.dma_start(offsets[:], offs)
-        load_row2(2048, T)
-        nc.vector.tensor_copy(place_of_row(2, LAST), row2[:].indirect(of_slice(LAST)))
-        for s in range(LAST):
-            gather_single(2, s)
-        load_pairs(0, 1536, 0)
-        load_pairs(1536, 2560, 0)
-        load_pairs(2560, T, (T - 2560) * 5 // 16)
-        for s in range(LAST):
-            gather_pairs(s)
-        for c0 in range(0, T, T // 4):
-            load_row3(c0, c0 + T // 4)
+        for d in range(4):
+            nc.sync.dma_start(out=rows[d][:], in_=x_rows[:, d, :])
+            if d == 0:
+                nc.sync.dma_start(offsets[:], offs)
+            gather_row(d)
+            if d == 1:
+                for s in range(SLICES):
+                    place(0, s, 0, SLICE)
 
         def load_scales(sources, e0, e1):
             for r in range(4):
@@ -158,17 +122,32 @@ def tile_moe_res_glu_gelu_kernel(
             load_words(w1_codes, w1_words, 2 * s, 2 * s + 2)
             load_words(w3_codes, w3_words, 2 * s, 2 * s + 2)
 
-        load_first_words(0)
-        load_scales(((w1_planes[0], w1_scales), (w3_planes[0], w3_scales)), 0, RUN)
-        load_first_words(1)
-        load_scales(((w2_plane, w2_scales),), 0, E)
-        load_words(w2_codes, w2_words, 0, RUN)
-        nc.sync.dma_start(out=gates[:, 0:SLICE], in_=gate[:, 0:SLICE])
-        load_scales(((w1_planes[1], w1_scales),), RUN, E)
-        load_scales(((w3_planes[1], w3_scales),), RUN, E)
+        def w2_and_gate():
+            load_scales(((w2_plane, w2_scales),), 0, E)
+            load_words(w2_codes, w2_words, 0, E)
+            nc.sync.dma_start(out=gates[:, 0:SLICE], in_=gate[:, 0:SLICE])
+
+        def late_scales():
+            if RUN < E:
+                load_scales(((w1_planes[1], w1_scales),), RUN, E)
+                load_scales(((w3_planes[1], w3_scales),), RUN, E)
+
+        load_words(w1_codes, w1_words, 0, 2)
+        load_scales(((w1_planes[0], w1_scales),), 0, RUN)
+        if LOADS % 2:
+            load_words(w1_codes, w1_words, 2, 4)
+        load_words(w3_codes, w3_words, 0, 2)
+        load_scales(((w3_planes[0], w3_scales),), 0, RUN)
+        if LOADS % 2 == 0:
+            load_words(w1_codes, w1_words, 2, 4)
+        load_words(w3_codes, w3_words, 2, 4)
+        if LOADS // 2:
+            w2_and_gate()
+        late_scales()
         load_first_words(2)
+        if LOADS // 2 == 0:
+            w2_and_gate()
         load_first_words(3)
-        load_words(w2_codes, w2_words, RUN, E)
         nc.sync.dma_start(out=gates[:, SLICE:S], in_=gate[:, SLICE:S])
         nc.sync.dma_start(out=residual[:], in_=xr)
 
@@ -177,28 +156,21 @@ def tile_moe_res_glu_gelu_kernel(
         results = [keep.tile([P, SLICE], F32, name=f"results{k}") for k in range(len(CUTS) - 1)]
         a_banks, b_banks, hiddens, turned, h_codes, h_scales, y_banks = ({} for kind in range(7))
 
-        def due_after(unit):
-            c = unit[-1] + GROUP_LAG
-            return c if c < ON_GPSIMD else max(c, CHUNKS - 1)
+        def units_of(k):
+            return [u for u, unit in enumerate(UNITS) if CUTS[k] <= unit[0] < CUTS[k + 1]]
 
+        shares = len(CUTS) - 1
         steps = []
-        for c in range(CHUNKS):
-            steps.append(("gate", c))
-            steps.extend(("group", u) for u, unit in enumerate(UNITS) if due_after(unit) == c)
-            if c in COLLECT_AFTER:
-                steps.append(("collect", COLLECT_AFTER.index(c)))
-        steps.extend(("group", u) for u, unit in enumerate(UNITS) if due_after(unit) >= CHUNKS)
-        steps.extend(("collect", k) for k in range(len(COLLECT_AFTER), len(CUTS) - 1))
+        for c in range(CHUNKS + 2):
+            if c < CHUNKS:
+                steps.append(("gate", c))
+            for k in range(shares):
+                if GROUP_AFTER[k] == c:
+                    steps.extend(("group", u) for u in units_of(k))
+            steps.extend(("collect", k) for k in range(shares) if COLLECT_AFTER[k] == c)
 
         def bank_of(step):
             return psum.tile([P, H], F32, name=f"step{steps.index(step) % RING}")
-
-        def quantise_tokens(s, first, last):
-            nc.vector.quantize_mx(
-                out=x_codes[s][:, first:last].bitcast(FP8X4),
-                scales=x_scales[s][:, first:last],
-                in_=grouped[s][:, 4 * first : 4 * last],
-            )
 
         def first_product(bank, c, codes, planes):
             e, s, at = c // 2, c // 4, (c % 4) * P
@@ -228,8 +200,8 @@ def tile_moe_res_glu_gelu_kernel(
             act = keep.tile([P, H], F32, name=f"act{c % TURN}")
             nc.scalar.activation(by_words(act), from_bank(a_banks[c]), GELU)
             hiddens[c] = keep.tile([P, H], BF16, name=f"hidden{c % TURN}", align_bytes=64)
-            if c == ON_GPSIMD:
-                up = keep.tile([P, H], F32, name="up_copy")
+            if c in ON_GPSIMD:
+                up = keep.tile([P, H], F32, name=f"up_copy{ON_GPSIMD.index(c) % UPS}")
                 nc.scalar.copy(out=by_words(up), in_=from_bank(b_banks[c]))
                 nc.gpsimd.tensor_tensor(hiddens[c][:], up[:], act[:], MULT)
             else:
@@ -247,10 +219,7 @@ def tile_moe_res_glu_gelu_kernel(
 
         def group_unit(u):
             count = len(UNITS[u])
-            if u == behind_row3:
-                h_grouped = singles[3][:, T : T + 4 * P * count]
-            else:
-                h_grouped = keep.tile([P, 4 * P * count], BF16, name=f"h_grouped{u}", align_bytes=64)[:]
+            h_grouped = keep.tile([P, 4 * P * count], BF16, name=f"h_grouped{u}", align_bytes=64)[:]
             nc.scalar.copy(
                 out=h_grouped.bitcast(F32).rearrange("p (c s u) -> p c s u", c=count, u=2),
                 in_=turned[u][:, 0 : 2 * P * count].rearrange("p (c u s) -> p c s u", c=count, u=2),
@@ -258,9 +227,6 @@ def tile_moe_res_glu_gelu_kernel(
             h_codes[u] = keep.tile([P, P * count], U32, name=f"h_codes{u}", align_bytes=64)
             h_scales[u] = keep.tile([P, P * count], U8, name=f"h_scales{u}", align_bytes=64)
             nc.vector.quantize_mx(out=h_codes[u][:].bitcast(FP8X4), scales=h_scales[u][:], in_=h_grouped)
-
-        def units_of(k):
-            return [u for u, unit in enumerate(UNITS) if CUTS[k] <= unit[0] < CUTS[k + 1]]
 
         def second_products(k):
             y_banks[k] = bank_of(("collect", k))
@@ -286,12 +252,19 @@ def tile_moe_res_glu_gelu_kernel(
                 MULT,
             )
 
-        gather_single(3, 0)
+        def quantise_tokens(s, first, last):
+            nc.vector.quantize_mx(
+                out=x_codes[s][:, first:last].bitcast(FP8X4),
+                scales=x_scales[s][:, first:last],
+                in_=grouped[s][:, 4 * first : 4 * last],
+            )
+
+        place(1, 0, 0, C)
+        place(1, 0, C, SLICE)
         quantise_tokens(0, 0, C)
         quantise_tokens(0, C, SLICE)
-        gather_pairs(LAST)
-        for s in range(1, LAST):
-            gather_single(3, s)
+        for s in range(1, SLICES):
+            place(1, s, 0, SLICE)
             quantise_tokens(s, 0, SLICE)
 
         def input_step(step):
@@ -309,9 +282,6 @@ def tile_moe_res_glu_gelu_kernel(
         filled = RING
         for at, (kind, n) in enumerate(steps):
             empty[kind](n)
-            if (kind, n) == ("collect", 0):
-                gather_single(3, LAST)
-                quantise_tokens(LAST, 0, SLICE)
             while filled < len(steps) and filled <= at + RING and steps.index(input_step(steps[filled])) <= at:
                 fill[steps[filled][0]](steps[filled][1])
                 filled = filled + 1

@@ -25,9 +25,9 @@ CHUNKS = S // P
 CUTS = (0, 3, 6, 10, 13, 16)
 UNIT_STARTS = sorted(set(range(0, CHUNKS, 2)) | set(CUTS))
 UNITS = [list(range(first, last)) for first, last in zip(UNIT_STARTS[:-1], UNIT_STARTS[1:])]
-ON_GPSIMD = (10, 13)
+ON_GPSIMD = (3, 7, 10, 13)
 UPS = 3
-GROUP_AFTER = (5, 9, 12, 15, 16)
+GROUP_AFTER = (7, 9, 12, 15, 16)
 COLLECT_AFTER = (9, 12, 15, 16, 17)
 LOADS = 0
 ON_VECTOR = (1024, 512, 768, 512)
@@ -122,31 +122,21 @@ def tile_moe_res_glu_gelu_kernel(
             load_words(w1_codes, w1_words, 2 * s, 2 * s + 2)
             load_words(w3_codes, w3_words, 2 * s, 2 * s + 2)
 
-        def w2_and_gate():
-            load_scales(((w2_plane, w2_scales),), 0, E)
-            load_words(w2_codes, w2_words, 0, E)
-            nc.sync.dma_start(out=gates[:, 0:SLICE], in_=gate[:, 0:SLICE])
-
-        def late_scales():
-            if RUN < E:
-                load_scales(((w1_planes[1], w1_scales),), RUN, E)
-                load_scales(((w3_planes[1], w3_scales),), RUN, E)
-
         load_words(w1_codes, w1_words, 0, 2)
-        load_scales(((w1_planes[0], w1_scales),), 0, RUN)
-        if LOADS % 2:
-            load_words(w1_codes, w1_words, 2, 4)
+        load_scales(((w1_planes[0], w1_scales),), 0, E)
+        load_words(w1_codes, w1_words, 2, 4)
+        load_scales(((w2_plane, w2_scales),), 0, E)
+        load_words(w2_codes, w2_words, 0, 4)
+        if LOADS == 1:
+            load_words(w1_codes, w1_words, 4, 6)
         load_words(w3_codes, w3_words, 0, 2)
-        load_scales(((w3_planes[0], w3_scales),), 0, RUN)
-        if LOADS % 2 == 0:
-            load_words(w1_codes, w1_words, 2, 4)
+        load_scales(((w3_planes[0], w3_scales),), 0, E)
         load_words(w3_codes, w3_words, 2, 4)
-        if LOADS // 2:
-            w2_and_gate()
-        late_scales()
-        load_first_words(2)
-        if LOADS // 2 == 0:
-            w2_and_gate()
+        if LOADS != 1:
+            load_words(w1_codes, w1_words, 4, 6)
+        load_words(w3_codes, w3_words, 4, 6)
+        nc.sync.dma_start(out=gates[:, 0:SLICE], in_=gate[:, 0:SLICE])
+        load_words(w2_codes, w2_words, 4, E)
         load_first_words(3)
         nc.sync.dma_start(out=gates[:, SLICE:S], in_=gate[:, SLICE:S])
         nc.sync.dma_start(out=residual[:], in_=xr)

@@ -25,11 +25,14 @@ CHUNKS = S // P
 CUTS = (0, 3, 6, 10, 13, 16)
 UNIT_STARTS = sorted(set(range(0, CHUNKS, 2)) | set(CUTS))
 UNITS = [list(range(first, last)) for first, last in zip(UNIT_STARTS[:-1], UNIT_STARTS[1:])]
-ON_GPSIMD = (3, 7, 10, 13)
+HAND_AFTER = {3: ("gate", 3), 6: ("group", 1), 10: ("gate", 10), 13: ("gate", 13)}
 UPS = 3
 GROUP_AFTER = (7, 9, 12, 15, 16)
 COLLECT_AFTER = (9, 12, 15, 16, 17)
 LOADS = 0
+AHEAD = 1
+EARLY = ()
+HELD = {6: 1}
 ON_VECTOR = (1024, 512, 768, 512)
 RING = 4
 TURN = 8
@@ -154,13 +157,18 @@ def tile_moe_res_glu_gelu_kernel(
         for c in range(CHUNKS + 2):
             if c < CHUNKS:
                 steps.append(("gate", c))
+            steps.extend(("collect", k) for k in EARLY if COLLECT_AFTER[k] == c)
             for k in range(shares):
                 if GROUP_AFTER[k] == c:
                     steps.extend(("group", u) for u in units_of(k))
-            steps.extend(("collect", k) for k in range(shares) if COLLECT_AFTER[k] == c)
+            steps.extend(("collect", k) for k in range(shares) if COLLECT_AFTER[k] == c and k not in EARLY)
+
+        banked = list(steps)
+        for c, after in HAND_AFTER.items():
+            steps.insert(steps.index(after) + 1, ("hand", c))
 
         def bank_of(step):
-            return psum.tile([P, H], F32, name=f"step{steps.index(step) % RING}")
+            return psum.tile([P, H], F32, name=f"step{banked.index(step) % RING}")
 
         def first_product(bank, c, codes, planes):
             e, s, at = c // 2, c // 4, (c % 4) * P
@@ -177,6 +185,8 @@ def tile_moe_res_glu_gelu_kernel(
         def first_products(c):
             a_banks[c] = bank_of(("gate", c))
             first_product(a_banks[c], c, w1_codes, w1_planes)
+
+        def up_product(c):
             b_banks[c] = psum.tile([P, H], F32, name=f"up{c % RING}")
             first_product(b_banks[c], c, w3_codes, w3_planes)
 
@@ -186,16 +196,34 @@ def tile_moe_res_glu_gelu_kernel(
         def by_words(tile):
             return tile[:].rearrange("s (u p e) -> s u p e", u=2, e=2)
 
+        acts = {}
+
+        free_ups = []
+
+        def multiplied(c):
+            free_ups.append(c + RING)
+
+        def fill_ups(upto):
+            for c in sorted(free_ups):
+                if c <= upto and c < CHUNKS:
+                    free_ups.remove(c)
+                    up_product(c)
+
         def gate_chunk(c):
-            act = keep.tile([P, H], F32, name=f"act{c % TURN}")
-            nc.scalar.activation(by_words(act), from_bank(a_banks[c]), GELU)
-            hiddens[c] = keep.tile([P, H], BF16, name=f"hidden{c % TURN}", align_bytes=64)
-            if c in ON_GPSIMD:
-                up = keep.tile([P, H], F32, name=f"up_copy{ON_GPSIMD.index(c) % UPS}")
-                nc.scalar.copy(out=by_words(up), in_=from_bank(b_banks[c]))
-                nc.gpsimd.tensor_tensor(hiddens[c][:], up[:], act[:], MULT)
-            else:
-                nc.vector.tensor_tensor(by_words(hiddens[c]), from_bank(b_banks[c]), by_words(act), MULT)
+            acts[c] = keep.tile([P, H], F32, name=f"act{c % TURN}")
+            nc.scalar.activation(by_words(acts[c]), from_bank(a_banks[c]), GELU)
+            if c not in HAND_AFTER:
+                hiddens[c] = keep.tile([P, H], BF16, name=f"hidden{c % TURN}", align_bytes=64)
+                nc.vector.tensor_tensor(by_words(hiddens[c]), from_bank(b_banks[c]), by_words(acts[c]), MULT)
+                multiplied(c)
+
+        def hand_over(c):
+            up = keep.tile([P, H], F32, name=f"up_copy{sorted(HAND_AFTER).index(c) % UPS}")
+            nc.scalar.copy(out=by_words(up), in_=from_bank(b_banks[c]))
+            name = f"h_grouped{HELD[c]}" if c in HELD else f"hidden{c % TURN}"
+            hiddens[c] = keep.tile([P, H], BF16, name=name, align_bytes=64)
+            nc.gpsimd.tensor_tensor(hiddens[c][:], up[:], acts[c][:], MULT)
+            multiplied(c)
 
         def turn(u):
             turned[u] = bank_of(("group", u))
@@ -253,28 +281,34 @@ def tile_moe_res_glu_gelu_kernel(
         place(1, 0, C, SLICE)
         quantise_tokens(0, 0, C)
         quantise_tokens(0, C, SLICE)
+        place(1, 1, 0, SLICE)
         for s in range(1, SLICES):
-            place(1, s, 0, SLICE)
+            if s + 1 < SLICES:
+                place(1, s + 1, 0, SLICE)
             quantise_tokens(s, 0, SLICE)
 
-        def input_step(step):
+        def inputs_written(step):
             kind, n = step
             if kind == "group":
-                return ("gate", UNITS[n][-1])
+                return all(c in hiddens for c in UNITS[n])
             if kind == "collect":
-                return ("group", units_of(n)[-1])
-            return steps[0]
+                return all(u in h_codes for u in units_of(n))
+            return True
 
         fill = {"gate": first_products, "group": turn, "collect": second_products}
-        empty = {"gate": gate_chunk, "group": group_unit, "collect": put_back}
-        for kind, n in steps[:RING]:
+        empty = {"gate": gate_chunk, "group": group_unit, "collect": put_back, "hand": hand_over}
+        for kind, n in banked[:RING]:
             fill[kind](n)
-        filled = RING
-        for at, (kind, n) in enumerate(steps):
+        for c in range(RING):
+            up_product(c)
+        filled, emptied = RING, 0
+        for kind, n in steps:
             empty[kind](n)
-            while filled < len(steps) and filled <= at + RING and steps.index(input_step(steps[filled])) <= at:
-                fill[steps[filled][0]](steps[filled][1])
+            emptied = emptied + (kind != "hand")
+            while filled < len(banked) and filled < emptied + RING and inputs_written(banked[filled]):
+                fill[banked[filled][0]](banked[filled][1])
                 filled = filled + 1
+            fill_ups(max(acts) + AHEAD)
 
         for c0 in range(0, T, STORE):
             c1 = min(c0 + STORE, T)

@@ -37,7 +37,7 @@ ON_VECTOR = (1024, 512, 768, 512)
 RING = 4
 TURN = 8
 RUN = 8
-STORE = 640
+STORE = 512
 FLOPS = 2 * S * (2 * K * H + H * N)
 
 
@@ -310,7 +310,7 @@ def tile_moe_res_glu_gelu_kernel(
                 filled = filled + 1
             fill_ups(max(acts) + AHEAD)
 
-        for c0 in range(0, T, STORE):
-            c1 = min(c0 + STORE, T)
+        cuts = [0] + list(range(STORE // 2, T, STORE)) + [T]
+        for c0, c1 in zip(cuts[:-1], cuts[1:]):
             nc.vector.tensor_tensor(residual[:, c0:c1], residual[:, c0:c1], scattered[:, c0:c1], ADD)
             nc.sync.dma_start(out=out[:, c0:c1], in_=residual[:, c0:c1])

@@ -25,15 +25,20 @@ CHUNKS = S // P
 CUTS = (0, 3, 6, 10, 13, 16)
 UNIT_STARTS = sorted(set(range(0, CHUNKS, 2)) | set(CUTS))
 UNITS = [list(range(first, last)) for first, last in zip(UNIT_STARTS[:-1], UNIT_STARTS[1:])]
-HAND_AFTER = {3: ("gate", 3), 6: ("group", 1), 10: ("gate", 10), 13: ("gate", 13)}
+HAND_AFTER = {7: ("group", 1), 10: ("gate", 10), 13: ("gate", 13)}
 UPS = 3
 GROUP_AFTER = (7, 9, 12, 15, 16)
 COLLECT_AFTER = (9, 12, 15, 16, 17)
-LOADS = 0
+LOADS = 2
+HOLD = 2
+LAST_QUANTISE = ("group", 1)
+LAST_SCALES = "h_grouped0"
+NARROW = (13,)
+LEFT = 32
 AHEAD = 1
 EARLY = ()
-HELD = {6: 1}
-ON_VECTOR = (1024, 512, 768, 512)
+HELD = {7: 1}
+ON_VECTOR = (1024, 512, 768, 384)
 RING = 4
 TURN = 8
 RUN = 8
@@ -53,7 +58,8 @@ def tile_moe_res_glu_gelu_kernel(
         psum = ctx.enter_context(tc.psum_pool(name="psum", bufs=1))
 
         offsets = keep.tile([P, S // 16], U16, name="offsets")
-        rows = [raw_pool.tile([P, T], F32, name=f"row{d}") for d in range(4)]
+        rows = [raw_pool.tile([P, T + (H if d == 3 else 0)], F32, name=f"row{d}") for d in range(4)]
+        behind_row3 = rows[3][:, T : T + H]
         picked = [[keep.tile([P, 2, SLICE], BF16, name=f"picked{u}_{s}") for s in range(SLICES)] for u in range(2)]
         grouped = [keep.tile([P, 4 * SLICE], BF16, name=f"grouped{s}", align_bytes=64) for s in range(SLICES)]
         w1_codes = keep.tile([P, E * 2 * H], U8, name="w1_codes", align_bytes=64)
@@ -73,6 +79,7 @@ def tile_moe_res_glu_gelu_kernel(
         for plane in w1_planes + w3_planes + [w2_plane]:
             nc.vector.memset(plane[:].bitcast(I32), 0)
         nc.vector.memset(scattered[:], 0.0)
+        nc.vector.memset(behind_row3, 0.0)
         make_identity(nc, identity[:])
 
         def entries(first, last):
@@ -87,18 +94,20 @@ def tile_moe_res_glu_gelu_kernel(
                 nc.scalar.activation(target, rows[d][:].indirect(entries(first, last)), COPY)
 
         def gather_row(d):
-            cuts = sorted(set(range(0, S + 1, SLICE)) | {ON_VECTOR[d]} | ({C} if d == 3 else set()))
+            cuts = sorted(set(range(0, S + 1, SLICE)) | {ON_VECTOR[d]} | ({C, S - P} if d == 3 else set()))
             for first, last in zip(cuts[:-1], cuts[1:]):
+                if d == 3 and first >= S - P:
+                    continue
                 gather(d, first, last, last <= ON_VECTOR[d])
 
         def place(u, s, first, last):
-            nc.vector.tensor_copy(
+            (nc.gpsimd if (u, s) == (1, SLICES - 1) else nc.vector).tensor_copy(
                 out=grouped[s][:].rearrange("p (t d) -> p t d", d=4)[:, first:last, 2 * u : 2 * u + 2],
                 in_=picked[u][s][:].rearrange("p d t -> p t d")[:, first:last, :],
             )
 
         for d in range(4):
-            nc.sync.dma_start(out=rows[d][:], in_=x_rows[:, d, :])
+            nc.sync.dma_start(out=rows[d][:, 0:T], in_=x_rows[:, d, :])
             if d == 0:
                 nc.sync.dma_start(offsets[:], offs)
             gather_row(d)
@@ -127,16 +136,24 @@ def tile_moe_res_glu_gelu_kernel(
 
         load_words(w1_codes, w1_words, 0, 2)
         load_scales(((w1_planes[0], w1_scales),), 0, E)
-        load_words(w1_codes, w1_words, 2, 4)
-        load_scales(((w2_plane, w2_scales),), 0, E)
-        load_words(w2_codes, w2_words, 0, 4)
-        if LOADS == 1:
-            load_words(w1_codes, w1_words, 4, 6)
+        def w2_first():
+            load_scales(((w2_plane, w2_scales),), 0, E)
+            load_words(w2_codes, w2_words, 0, 4)
+
+        if LOADS == 0:
+            load_words(w1_codes, w1_words, 2, 4)
+        if LOADS in (0, 3):
+            w2_first()
         load_words(w3_codes, w3_words, 0, 2)
         load_scales(((w3_planes[0], w3_scales),), 0, E)
+        if LOADS != 0:
+            load_words(w1_codes, w1_words, 2, 4)
         load_words(w3_codes, w3_words, 2, 4)
-        if LOADS != 1:
-            load_words(w1_codes, w1_words, 4, 6)
+        if LOADS == 1:
+            w2_first()
+        load_words(w1_codes, w1_words, 4, 6)
+        if LOADS == 2:
+            w2_first()
         load_words(w3_codes, w3_words, 4, 6)
         nc.sync.dma_start(out=gates[:, 0:SLICE], in_=gate[:, 0:SLICE])
         load_words(w2_codes, w2_words, 4, E)
@@ -145,7 +162,7 @@ def tile_moe_res_glu_gelu_kernel(
         nc.sync.dma_start(out=residual[:], in_=xr)
 
         x_codes = [keep.tile([P, SLICE], U32, name=f"x_codes{s}", align_bytes=64) for s in range(SLICES)]
-        x_scales = [keep.tile([P, SLICE], U8, name=f"x_scales{s}", align_bytes=64) for s in range(SLICES)]
+        x_scales = [keep.tile([P, SLICE], U8, name=f"x_scales{s}", align_bytes=64) for s in range(SLICES - 1)]
         results = [keep.tile([P, SLICE], F32, name=f"results{k}") for k in range(len(CUTS) - 1)]
         a_banks, b_banks, hiddens, turned, h_codes, h_scales, y_banks = ({} for kind in range(7))
 
@@ -210,7 +227,7 @@ def tile_moe_res_glu_gelu_kernel(
                     up_product(c)
 
         def gate_chunk(c):
-            acts[c] = keep.tile([P, H], F32, name=f"act{c % TURN}")
+            acts[c] = behind_row3 if c == HOLD else keep.tile([P, H], F32, name=f"act{c % TURN}")
             nc.scalar.activation(by_words(acts[c]), from_bank(a_banks[c]), GELU)
             if c not in HAND_AFTER:
                 hiddens[c] = keep.tile([P, H], BF16, name=f"hidden{c % TURN}", align_bytes=64)
@@ -222,7 +239,15 @@ def tile_moe_res_glu_gelu_kernel(
             nc.scalar.copy(out=by_words(up), in_=from_bank(b_banks[c]))
             name = f"h_grouped{HELD[c]}" if c in HELD else f"hidden{c % TURN}"
             hiddens[c] = keep.tile([P, H], BF16, name=name, align_bytes=64)
-            nc.gpsimd.tensor_tensor(hiddens[c][:], up[:], acts[c][:], MULT)
+            share = H if c not in NARROW else H - 2 * LEFT
+            nc.gpsimd.tensor_tensor(hiddens[c][:, 0:share], up[:, 0:share], acts[c][:, 0:share], MULT)
+            if share < H:
+                nc.vector.tensor_tensor(
+                    by_words(hiddens[c])[:, 1, P - LEFT : P],
+                    from_bank(b_banks[c])[:, 1, P - LEFT : P],
+                    by_words(acts[c])[:, 1, P - LEFT : P],
+                    MULT,
+                )
             multiplied(c)
 
         def turn(u):
@@ -271,6 +296,8 @@ def tile_moe_res_glu_gelu_kernel(
             )
 
         def quantise_tokens(s, first, last):
+            if s == SLICES - 1:
+                x_scales.append(keep.tile([P, SLICE], U8, name=LAST_SCALES, align_bytes=64))
             nc.vector.quantize_mx(
                 out=x_codes[s][:, first:last].bitcast(FP8X4),
                 scales=x_scales[s][:, first:last],
@@ -282,8 +309,8 @@ def tile_moe_res_glu_gelu_kernel(
         quantise_tokens(0, 0, C)
         quantise_tokens(0, C, SLICE)
         place(1, 1, 0, SLICE)
-        for s in range(1, SLICES):
-            if s + 1 < SLICES:
+        for s in range(1, SLICES - 1):
+            if s + 2 < SLICES:
                 place(1, s + 1, 0, SLICE)
             quantise_tokens(s, 0, SLICE)
 
@@ -304,6 +331,11 @@ def tile_moe_res_glu_gelu_kernel(
         filled, emptied = RING, 0
         for kind, n in steps:
             empty[kind](n)
+            if (kind, n) == ("gate", HOLD):
+                gather(3, S - P, S, False)
+                place(1, SLICES - 1, 0, SLICE)
+            if (kind, n) == LAST_QUANTISE:
+                quantise_tokens(SLICES - 1, 0, SLICE)
             emptied = emptied + (kind != "hand")
             while filled < len(banked) and filled < emptied + RING and inputs_written(banked[filled]):
                 fill[banked[filled][0]](banked[filled][1])

@@ -22,26 +22,17 @@ S = E * C
 SLICE = 512
 SLICES = S // SLICE
 CHUNKS = S // P
+LAST = SLICES - 1
+ON_VECTOR = (1024, 512, 768, 256)
 CUTS = (0, 3, 6, 10, 13, 16)
+SHARES = len(CUTS) - 1
 UNIT_STARTS = sorted(set(range(0, CHUNKS, 2)) | set(CUTS))
 UNITS = [list(range(first, last)) for first, last in zip(UNIT_STARTS[:-1], UNIT_STARTS[1:])]
-HAND_AFTER = {7: ("group", 1), 10: ("gate", 10), 13: ("gate", 13)}
-UPS = 3
-GROUP_AFTER = (7, 9, 12, 15, 16)
-COLLECT_AFTER = (9, 12, 15, 16, 17)
-LOADS = 2
-HOLD = 2
-LAST_QUANTISE = ("group", 1)
-LAST_SCALES = "h_grouped0"
-NARROW = (13,)
-LEFT = 32
-AHEAD = 1
-EARLY = ()
-HELD = {7: 1}
-ON_VECTOR = (1024, 512, 768, 384)
 RING = 4
+AHEAD = 2 * RING
+ON_GPSIMD = (AHEAD - 1,) + CUTS[-3:-1]
+LEFT = 32
 TURN = 8
-RUN = 8
 STORE = 512
 FLOPS = 2 * S * (2 * K * H + H * N)
 
@@ -65,8 +56,8 @@ def tile_moe_res_glu_gelu_kernel(
         w1_codes = keep.tile([P, E * 2 * H], U8, name="w1_codes", align_bytes=64)
         w3_codes = keep.tile([P, E * 2 * H], U8, name="w3_codes", align_bytes=64)
         w2_codes = keep.tile([P, E * 2 * N], U8, name="w2_codes", align_bytes=64)
-        w1_planes = [keep.tile([P, RUN * H], U8, name=f"w1_plane{r}", align_bytes=64) for r in range(E // RUN)]
-        w3_planes = [keep.tile([P, RUN * H], U8, name=f"w3_plane{r}", align_bytes=64) for r in range(E // RUN)]
+        w1_plane = keep.tile([P, E * H], U8, name="w1_plane0", align_bytes=64)
+        w3_plane = keep.tile([P, E * H], U8, name="w3_plane0", align_bytes=64)
         w2_plane = keep.tile([P, E * N], U8, name="w2_plane", align_bytes=64)
         gates = keep.tile([P, S], F32, name="gates")
         residual = keep.tile([P, T], F32, name="residual")
@@ -76,7 +67,7 @@ def tile_moe_res_glu_gelu_kernel(
 
         nc.vector.memset(warm[:], 0.0)
         nc.scalar.activation(warm[:], warm[:], GELU)
-        for plane in w1_planes + w3_planes + [w2_plane]:
+        for plane in (w1_plane, w3_plane, w2_plane):
             nc.vector.memset(plane[:].bitcast(I32), 0)
         nc.vector.memset(scattered[:], 0.0)
         nc.vector.memset(behind_row3, 0.0)
@@ -93,15 +84,8 @@ def tile_moe_res_glu_gelu_kernel(
             else:
                 nc.scalar.activation(target, rows[d][:].indirect(entries(first, last)), COPY)
 
-        def gather_row(d):
-            cuts = sorted(set(range(0, S + 1, SLICE)) | {ON_VECTOR[d]} | ({C, S - P} if d == 3 else set()))
-            for first, last in zip(cuts[:-1], cuts[1:]):
-                if d == 3 and first >= S - P:
-                    continue
-                gather(d, first, last, last <= ON_VECTOR[d])
-
-        def place(u, s, first, last):
-            (nc.gpsimd if (u, s) == (1, SLICES - 1) else nc.vector).tensor_copy(
+        def place(engine, u, s, first, last):
+            engine.tensor_copy(
                 out=grouped[s][:].rearrange("p (t d) -> p t d", d=4)[:, first:last, 2 * u : 2 * u + 2],
                 in_=picked[u][s][:].rearrange("p d t -> p t d")[:, first:last, :],
             )
@@ -110,18 +94,19 @@ def tile_moe_res_glu_gelu_kernel(
             nc.sync.dma_start(out=rows[d][:, 0:T], in_=x_rows[:, d, :])
             if d == 0:
                 nc.sync.dma_start(offsets[:], offs)
-            gather_row(d)
+            cuts = sorted(set(range(0, S, SLICE)) | {ON_VECTOR[d], S - P if d == 3 else S})
+            for first, last in zip(cuts[:-1], cuts[1:]):
+                gather(d, first, last, last <= ON_VECTOR[d])
             if d == 1:
                 for s in range(SLICES):
-                    place(0, s, 0, SLICE)
+                    place(nc.vector, 0, s, 0, SLICE)
 
-        def load_scales(sources, e0, e1):
+        def load_scales(plane, scales):
             for r in range(4):
-                for plane, scales in sources:
-                    nc.sync.dma_start(
-                        out=plane[r:P:32, :].bitcast(I32).rearrange("q (e i) -> q e i", e=e1 - e0),
-                        in_=scales[e0:e1].rearrange("e s (q r) i -> r q (e s) i", r=4)[r].bitcast(I32),
-                    )
+                nc.sync.dma_start(
+                    out=plane[r:P:32, :].bitcast(I32).rearrange("q (e i) -> q e i", e=E),
+                    in_=scales.rearrange("e s (q r) i -> r q (e s) i", r=4)[r].bitcast(I32),
+                )
 
         def load_words(codes, words, e0, e1):
             wide = words.shape[3]
@@ -130,82 +115,67 @@ def tile_moe_res_glu_gelu_kernel(
                 in_=words[e0:e1].rearrange("e s p b -> p (e s) b").bitcast(I32),
             )
 
-        def load_first_words(s):
-            load_words(w1_codes, w1_words, 2 * s, 2 * s + 2)
-            load_words(w3_codes, w3_words, 2 * s, 2 * s + 2)
-
         load_words(w1_codes, w1_words, 0, 2)
-        load_scales(((w1_planes[0], w1_scales),), 0, E)
-        def w2_first():
-            load_scales(((w2_plane, w2_scales),), 0, E)
-            load_words(w2_codes, w2_words, 0, 4)
-
-        if LOADS == 0:
-            load_words(w1_codes, w1_words, 2, 4)
-        if LOADS in (0, 3):
-            w2_first()
+        load_scales(w1_plane, w1_scales)
         load_words(w3_codes, w3_words, 0, 2)
-        load_scales(((w3_planes[0], w3_scales),), 0, E)
-        if LOADS != 0:
-            load_words(w1_codes, w1_words, 2, 4)
+        load_scales(w3_plane, w3_scales)
+        load_words(w1_codes, w1_words, 2, 4)
         load_words(w3_codes, w3_words, 2, 4)
-        if LOADS == 1:
-            w2_first()
         load_words(w1_codes, w1_words, 4, 6)
-        if LOADS == 2:
-            w2_first()
+        load_scales(w2_plane, w2_scales)
+        load_words(w2_codes, w2_words, 0, 4)
         load_words(w3_codes, w3_words, 4, 6)
         nc.sync.dma_start(out=gates[:, 0:SLICE], in_=gate[:, 0:SLICE])
         load_words(w2_codes, w2_words, 4, E)
-        load_first_words(3)
+        load_words(w1_codes, w1_words, 6, E)
+        load_words(w3_codes, w3_words, 6, E)
         nc.sync.dma_start(out=gates[:, SLICE:S], in_=gate[:, SLICE:S])
         nc.sync.dma_start(out=residual[:], in_=xr)
 
         x_codes = [keep.tile([P, SLICE], U32, name=f"x_codes{s}", align_bytes=64) for s in range(SLICES)]
-        x_scales = [keep.tile([P, SLICE], U8, name=f"x_scales{s}", align_bytes=64) for s in range(SLICES - 1)]
-        results = [keep.tile([P, SLICE], F32, name=f"results{k}") for k in range(len(CUTS) - 1)]
-        a_banks, b_banks, hiddens, turned, h_codes, h_scales, y_banks = ({} for kind in range(7))
+        x_scales = [keep.tile([P, SLICE], U8, name=f"x_scales{s}", align_bytes=64) for s in range(LAST)]
+        results = [keep.tile([P, SLICE], F32, name=f"results{k}") for k in range(SHARES)]
+        a_banks, b_banks, acts, hiddens, turned, h_codes, h_scales, y_banks = ({} for kind in range(8))
 
         def units_of(k):
             return [u for u, unit in enumerate(UNITS) if CUTS[k] <= unit[0] < CUTS[k + 1]]
 
-        shares = len(CUTS) - 1
-        steps = []
-        for c in range(CHUNKS + 2):
-            if c < CHUNKS:
-                steps.append(("gate", c))
-            steps.extend(("collect", k) for k in EARLY if COLLECT_AFTER[k] == c)
-            for k in range(shares):
-                if GROUP_AFTER[k] == c:
-                    steps.extend(("group", u) for u in units_of(k))
-            steps.extend(("collect", k) for k in range(shares) if COLLECT_AFTER[k] == c and k not in EARLY)
-
-        banked = list(steps)
-        for c, after in HAND_AFTER.items():
+        banked = []
+        for k in range(1, SHARES + 1):
+            gelus = max(CUTS[min(k + 1, SHARES)], AHEAD)
+            banked.extend(("gate", c) for c in range(gelus) if ("gate", c) not in banked)
+            banked.extend(("group", u) for u in units_of(k - 1))
+            if k >= 2:
+                banked.append(("collect", k - 2))
+        banked.append(("collect", SHARES - 1))
+        held_chunk, holding_unit = ON_GPSIMD[0], units_of(0)[-1]
+        steps = list(banked)
+        for c in ON_GPSIMD:
+            after = ("group", holding_unit) if c == held_chunk else ("gate", c)
             steps.insert(steps.index(after) + 1, ("hand", c))
 
         def bank_of(step):
             return psum.tile([P, H], F32, name=f"step{banked.index(step) % RING}")
 
-        def first_product(bank, c, codes, planes):
+        def first_product(bank, c, codes, plane):
             e, s, at = c // 2, c // 4, (c % 4) * P
             nc.tensor.matmul_mx(
                 out=bank[:],
                 lhsT=x_codes[s][:, at : at + P].bitcast(FP8X4),
                 lhsT_scale=x_scales[s][:, at : at + P],
                 rhs=codes[:, e * 2 * H : (e + 1) * 2 * H].bitcast(FP4X4),
-                rhs_scale=planes[e // RUN][:, (e % RUN) * H : (e % RUN + 1) * H],
+                rhs_scale=plane[:, e * H : (e + 1) * H],
                 start=True,
                 stop=True,
             )
 
-        def first_products(c):
+        def gate_product(c):
             a_banks[c] = bank_of(("gate", c))
-            first_product(a_banks[c], c, w1_codes, w1_planes)
+            first_product(a_banks[c], c, w1_codes, w1_plane)
 
         def up_product(c):
             b_banks[c] = psum.tile([P, H], F32, name=f"up{c % RING}")
-            first_product(b_banks[c], c, w3_codes, w3_planes)
+            first_product(b_banks[c], c, w3_codes, w3_plane)
 
         def from_bank(bank):
             return bank[:].rearrange("s (p u e) -> s u p e", u=2, e=2)
@@ -213,52 +183,46 @@ def tile_moe_res_glu_gelu_kernel(
         def by_words(tile):
             return tile[:].rearrange("s (u p e) -> s u p e", u=2, e=2)
 
-        acts = {}
-
-        free_ups = []
-
-        def multiplied(c):
-            free_ups.append(c + RING)
-
-        def fill_ups(upto):
-            for c in sorted(free_ups):
-                if c <= upto and c < CHUNKS:
-                    free_ups.remove(c)
-                    up_product(c)
-
         def gate_chunk(c):
-            acts[c] = behind_row3 if c == HOLD else keep.tile([P, H], F32, name=f"act{c % TURN}")
+            acts[c] = behind_row3 if c == 0 else keep.tile([P, H], F32, name=f"act{c % TURN}")
             nc.scalar.activation(by_words(acts[c]), from_bank(a_banks[c]), GELU)
-            if c not in HAND_AFTER:
+            if c not in ON_GPSIMD:
                 hiddens[c] = keep.tile([P, H], BF16, name=f"hidden{c % TURN}", align_bytes=64)
                 nc.vector.tensor_tensor(by_words(hiddens[c]), from_bank(b_banks[c]), by_words(acts[c]), MULT)
-                multiplied(c)
+            if c == 0:
+                gather(3, S - P, S, True)
+                place(nc.gpsimd, 1, LAST, 0, SLICE)
 
         def hand_over(c):
-            up = keep.tile([P, H], F32, name=f"up_copy{sorted(HAND_AFTER).index(c) % UPS}")
-            nc.scalar.copy(out=by_words(up), in_=from_bank(b_banks[c]))
-            name = f"h_grouped{HELD[c]}" if c in HELD else f"hidden{c % TURN}"
+            up = keep.tile([P, H], F32, name=f"up_copy{ON_GPSIMD.index(c)}")
+            words = P - LEFT
+            nc.scalar.copy(out=by_words(up)[:, 0], in_=from_bank(b_banks[c])[:, 0])
+            nc.scalar.copy(out=by_words(up)[:, 1, 0:words], in_=from_bank(b_banks[c])[:, 1, 0:words])
+            name = f"h_grouped{holding_unit}" if c == held_chunk else f"hidden{c % TURN}"
             hiddens[c] = keep.tile([P, H], BF16, name=name, align_bytes=64)
-            share = H if c not in NARROW else H - 2 * LEFT
-            nc.gpsimd.tensor_tensor(hiddens[c][:, 0:share], up[:, 0:share], acts[c][:, 0:share], MULT)
-            if share < H:
-                nc.vector.tensor_tensor(
-                    by_words(hiddens[c])[:, 1, P - LEFT : P],
-                    from_bank(b_banks[c])[:, 1, P - LEFT : P],
-                    by_words(acts[c])[:, 1, P - LEFT : P],
-                    MULT,
-                )
-            multiplied(c)
+            columns = 2 * (P + words)
+            nc.gpsimd.tensor_tensor(hiddens[c][:, 0:columns], up[:, 0:columns], acts[c][:, 0:columns], MULT)
+            nc.vector.tensor_tensor(
+                by_words(hiddens[c])[:, 1, words:P],
+                from_bank(b_banks[c])[:, 1, words:P],
+                by_words(acts[c])[:, 1, words:P],
+                MULT,
+            )
 
         def turn(u):
             turned[u] = bank_of(("group", u))
             for n, c in enumerate(UNITS[u]):
                 words = hiddens[c][:].bitcast(F32)
                 for half in range(2):
-                    place = (2 * n + half) * P
-                    nc.tensor.transpose(
-                        turned[u][:, place : place + P], words[:, half * P : (half + 1) * P], identity[:]
-                    )
+                    at = (2 * n + half) * P
+                    nc.tensor.transpose(turned[u][:, at : at + P], words[:, half * P : (half + 1) * P], identity[:])
+
+        def quantise_tokens(s, first, last):
+            nc.vector.quantize_mx(
+                out=x_codes[s][:, first:last].bitcast(FP8X4),
+                scales=x_scales[s][:, first:last],
+                in_=grouped[s][:, 4 * first : 4 * last],
+            )
 
         def group_unit(u):
             count = len(UNITS[u])
@@ -270,6 +234,9 @@ def tile_moe_res_glu_gelu_kernel(
             h_codes[u] = keep.tile([P, P * count], U32, name=f"h_codes{u}", align_bytes=64)
             h_scales[u] = keep.tile([P, P * count], U8, name=f"h_scales{u}", align_bytes=64)
             nc.vector.quantize_mx(out=h_codes[u][:].bitcast(FP8X4), scales=h_scales[u][:], in_=h_grouped)
+            if u == holding_unit:
+                x_scales.append(keep.tile([P, SLICE], U8, name="h_grouped0", align_bytes=64))
+                quantise_tokens(LAST, 0, SLICE)
 
         def second_products(k):
             y_banks[k] = bank_of(("collect", k))
@@ -295,23 +262,13 @@ def tile_moe_res_glu_gelu_kernel(
                 MULT,
             )
 
-        def quantise_tokens(s, first, last):
-            if s == SLICES - 1:
-                x_scales.append(keep.tile([P, SLICE], U8, name=LAST_SCALES, align_bytes=64))
-            nc.vector.quantize_mx(
-                out=x_codes[s][:, first:last].bitcast(FP8X4),
-                scales=x_scales[s][:, first:last],
-                in_=grouped[s][:, 4 * first : 4 * last],
-            )
-
-        place(1, 0, 0, C)
-        place(1, 0, C, SLICE)
+        place(nc.vector, 1, 0, 0, C)
+        place(nc.vector, 1, 0, C, SLICE)
         quantise_tokens(0, 0, C)
         quantise_tokens(0, C, SLICE)
-        place(1, 1, 0, SLICE)
-        for s in range(1, SLICES - 1):
-            if s + 2 < SLICES:
-                place(1, s + 1, 0, SLICE)
+        for s in range(1, LAST):
+            place(nc.vector, 1, s, 0, SLICE)
+        for s in range(1, LAST):
             quantise_tokens(s, 0, SLICE)
 
         def inputs_written(step):
@@ -322,7 +279,7 @@ def tile_moe_res_glu_gelu_kernel(
                 return all(u in h_codes for u in units_of(n))
             return True
 
-        fill = {"gate": first_products, "group": turn, "collect": second_products}
+        fill = {"gate": gate_product, "group": turn, "collect": second_products}
         empty = {"gate": gate_chunk, "group": group_unit, "collect": put_back, "hand": hand_over}
         for kind, n in banked[:RING]:
             fill[kind](n)
@@ -331,16 +288,13 @@ def tile_moe_res_glu_gelu_kernel(
         filled, emptied = RING, 0
         for kind, n in steps:
             empty[kind](n)
-            if (kind, n) == ("gate", HOLD):
-                gather(3, S - P, S, False)
-                place(1, SLICES - 1, 0, SLICE)
-            if (kind, n) == LAST_QUANTISE:
-                quantise_tokens(SLICES - 1, 0, SLICE)
             emptied = emptied + (kind != "hand")
             while filled < len(banked) and filled < emptied + RING and inputs_written(banked[filled]):
                 fill[banked[filled][0]](banked[filled][1])
                 filled = filled + 1
-            fill_ups(max(acts) + AHEAD)
+            for c in range(RING, min(max(acts) + 2, CHUNKS)):
+                if c not in b_banks and c - RING in hiddens:
+                    up_product(c)
 
         cuts = [0] + list(range(STORE // 2, T, STORE)) + [T]
         for c0, c1 in zip(cuts[:-1], cuts[1:]):

@@ -34,6 +34,7 @@ ON_GPSIMD = (AHEAD - 1,) + CUTS[-3:-1]
 LEFT = 32
 TURN = 8
 STORE = 512
+FIRST = 2
 FLOPS = 2 * S * (2 * K * H + H * N)
 
 
@@ -56,8 +57,8 @@ def tile_moe_res_glu_gelu_kernel(
         w1_codes = keep.tile([P, E * 2 * H], U8, name="w1_codes", align_bytes=64)
         w3_codes = keep.tile([P, E * 2 * H], U8, name="w3_codes", align_bytes=64)
         w2_codes = keep.tile([P, E * 2 * N], U8, name="w2_codes", align_bytes=64)
-        w1_plane = keep.tile([P, E * H], U8, name="w1_plane0", align_bytes=64)
-        w3_plane = keep.tile([P, E * H], U8, name="w3_plane0", align_bytes=64)
+        w1_plane = [keep.tile([P, n * H], U8, name=f"w1_plane{n}", align_bytes=64) for n in (FIRST, E - FIRST)]
+        w3_plane = [keep.tile([P, n * H], U8, name=f"w3_plane{n}", align_bytes=64) for n in (FIRST, E - FIRST)]
         w2_plane = keep.tile([P, E * N], U8, name="w2_plane", align_bytes=64)
         gates = keep.tile([P, S], F32, name="gates")
         residual = keep.tile([P, T], F32, name="residual")
@@ -67,7 +68,7 @@ def tile_moe_res_glu_gelu_kernel(
 
         nc.vector.memset(warm[:], 0.0)
         nc.scalar.activation(warm[:], warm[:], GELU)
-        for plane in (w1_plane, w3_plane, w2_plane):
+        for plane in w1_plane + w3_plane + [w2_plane]:
             nc.vector.memset(plane[:].bitcast(I32), 0)
         nc.vector.memset(scattered[:], 0.0)
         nc.vector.memset(behind_row3, 0.0)
@@ -101,11 +102,11 @@ def tile_moe_res_glu_gelu_kernel(
                 for s in range(SLICES):
                     place(nc.vector, 0, s, 0, SLICE)
 
-        def load_scales(plane, scales):
+        def load_scales(plane, scales, e0, e1):
             for r in range(4):
                 nc.sync.dma_start(
-                    out=plane[r:P:32, :].bitcast(I32).rearrange("q (e i) -> q e i", e=E),
-                    in_=scales.rearrange("e s (q r) i -> r q (e s) i", r=4)[r].bitcast(I32),
+                    out=plane[r:P:32, :].bitcast(I32).rearrange("q (e i) -> q e i", e=e1 - e0),
+                    in_=scales[e0:e1].rearrange("e s (q r) i -> r q (e s) i", r=4)[r].bitcast(I32),
                 )
 
         def load_words(codes, words, e0, e1):
@@ -116,15 +117,17 @@ def tile_moe_res_glu_gelu_kernel(
             )
 
         load_words(w1_codes, w1_words, 0, 2)
-        load_scales(w1_plane, w1_scales)
+        load_scales(w1_plane[0], w1_scales, 0, FIRST)
         load_words(w3_codes, w3_words, 0, 2)
-        load_scales(w3_plane, w3_scales)
+        load_scales(w3_plane[0], w3_scales, 0, FIRST)
+        load_scales(w1_plane[1], w1_scales, FIRST, E)
+        load_scales(w3_plane[1], w3_scales, FIRST, E)
         load_words(w1_codes, w1_words, 2, 4)
         load_words(w3_codes, w3_words, 2, 4)
         load_words(w1_codes, w1_words, 4, 6)
-        load_scales(w2_plane, w2_scales)
-        load_words(w2_codes, w2_words, 0, 4)
         load_words(w3_codes, w3_words, 4, 6)
+        load_scales(w2_plane, w2_scales, 0, E)
+        load_words(w2_codes, w2_words, 0, 4)
         nc.sync.dma_start(out=gates[:, 0:SLICE], in_=gate[:, 0:SLICE])
         load_words(w2_codes, w2_words, 4, E)
         load_words(w1_codes, w1_words, 6, E)
@@ -164,7 +167,7 @@ def tile_moe_res_glu_gelu_kernel(
                 lhsT=x_codes[s][:, at : at + P].bitcast(FP8X4),
                 lhsT_scale=x_scales[s][:, at : at + P],
                 rhs=codes[:, e * 2 * H : (e + 1) * 2 * H].bitcast(FP4X4),
-                rhs_scale=plane[:, e * H : (e + 1) * H],
+                rhs_scale=plane[0][:, e * H : (e + 1) * H] if e < FIRST else plane[1][:, (e - FIRST) * H : (e - FIRST + 1) * H],
                 start=True,
                 stop=True,
             )

@@ -187,12 +187,12 @@ def tile_moe_res_glu_gelu_kernel(
             return tile[:].rearrange("s (u p e) -> s u p e", u=2, e=2)
 
         def gate_chunk(c):
-            acts[c] = behind_row3 if c == 0 else keep.tile([P, H], F32, name=f"act{c % TURN}")
+            acts[c] = behind_row3 if c == 1 else keep.tile([P, H], F32, name=f"act{c % TURN}")
             nc.scalar.activation(by_words(acts[c]), from_bank(a_banks[c]), GELU)
             if c not in ON_GPSIMD:
                 hiddens[c] = keep.tile([P, H], BF16, name=f"hidden{c % TURN}", align_bytes=64)
                 nc.vector.tensor_tensor(by_words(hiddens[c]), from_bank(b_banks[c]), by_words(acts[c]), MULT)
-            if c == 0:
+            if c == 1:
                 gather(3, S - P, S, True)
                 place(nc.gpsimd, 1, LAST, 0, SLICE)
 
@@ -201,7 +201,7 @@ def tile_moe_res_glu_gelu_kernel(
             words = P - LEFT
             nc.scalar.copy(out=by_words(up)[:, 0], in_=from_bank(b_banks[c])[:, 0])
             nc.scalar.copy(out=by_words(up)[:, 1, 0:words], in_=from_bank(b_banks[c])[:, 1, 0:words])
-            name = f"h_grouped{holding_unit}" if c == held_chunk else f"hidden{c % TURN}"
+            name = f"h_grouped{units_of(ON_GPSIMD.index(c))[-1]}"
             hiddens[c] = keep.tile([P, H], BF16, name=name, align_bytes=64)
             columns = 2 * (P + words)
             nc.gpsimd.tensor_tensor(hiddens[c][:, 0:columns], up[:, 0:columns], acts[c][:, 0:columns], MULT)
@@ -295,7 +295,7 @@ def tile_moe_res_glu_gelu_kernel(
             while filled < len(banked) and filled < emptied + RING and inputs_written(banked[filled]):
                 fill[banked[filled][0]](banked[filled][1])
                 filled = filled + 1
-            for c in range(RING, min(max(acts) + 2, CHUNKS)):
+            for c in range(RING, min(max(acts) + 3, CHUNKS)):
                 if c not in b_banks and c - RING in hiddens:
                     up_product(c)
 

@@ -23,7 +23,7 @@ SLICE = 512
 SLICES = S // SLICE
 CHUNKS = S // P
 LAST = SLICES - 1
-ON_VECTOR = (1024, 512, 768, 256)
+ON_VECTOR = (1024, 512, 896, 384)
 CUTS = (0, 3, 6, 10, 13, 16)
 SHARES = len(CUTS) - 1
 UNIT_STARTS = sorted(set(range(0, CHUNKS, 2)) | set(CUTS))
@@ -52,7 +52,8 @@ def tile_moe_res_glu_gelu_kernel(
         offsets = keep.tile([P, S // 16], U16, name="offsets")
         rows = [raw_pool.tile([P, T + (H if d == 3 else 0)], F32, name=f"row{d}") for d in range(4)]
         behind_row3 = rows[3][:, T : T + H]
-        picked = [[keep.tile([P, 2, SLICE], BF16, name=f"picked{u}_{s}") for s in range(SLICES)] for u in range(2)]
+        picked = [[keep.tile([P, 2, SLICE], BF16, name=f"picked{u}_{s}") for s in range(LAST)] for u in range(2)]
+        picked_last = keep.tile([P, 4, SLICE], BF16, name="picked_last")
         grouped = [keep.tile([P, 4 * SLICE], BF16, name=f"grouped{s}", align_bytes=64) for s in range(SLICES)]
         w1_codes = keep.tile([P, E * 2 * H], U8, name="w1_codes", align_bytes=64)
         w3_codes = keep.tile([P, E * 2 * H], U8, name="w3_codes", align_bytes=64)
@@ -79,7 +80,8 @@ def tile_moe_res_glu_gelu_kernel(
 
         def gather(d, first, last, on_vector):
             s, at = first // SLICE, first % SLICE
-            target = picked[d // 2][s][:, d % 2, at : at + last - first]
+            row = picked_last[:, d] if s == LAST else picked[d // 2][s][:, d % 2]
+            target = row[:, at : at + last - first]
             if on_vector:
                 nc.vector.tensor_copy(target, rows[d][:].indirect(entries(first, last)))
             else:
@@ -95,11 +97,11 @@ def tile_moe_res_glu_gelu_kernel(
             nc.sync.dma_start(out=rows[d][:, 0:T], in_=x_rows[:, d, :])
             if d == 0:
                 nc.sync.dma_start(offsets[:], offs)
-            cuts = sorted(set(range(0, S, SLICE)) | {ON_VECTOR[d], S - P if d == 3 else S})
+            cuts = sorted(set(range(0, S, SLICE)) | {ON_VECTOR[d]} | ({C, S - P} if d == 3 else {S}))
             for first, last in zip(cuts[:-1], cuts[1:]):
                 gather(d, first, last, last <= ON_VECTOR[d])
             if d == 1:
-                for s in range(SLICES):
+                for s in range(LAST):
                     place(nc.vector, 0, s, 0, SLICE)
 
         def load_scales(plane, scales, e0, e1):
@@ -194,7 +196,14 @@ def tile_moe_res_glu_gelu_kernel(
                 nc.vector.tensor_tensor(by_words(hiddens[c]), from_bank(b_banks[c]), by_words(acts[c]), MULT)
             if c == 1:
                 gather(3, S - P, S, True)
-                place(nc.gpsimd, 1, LAST, 0, SLICE)
+                nc.gpsimd.tensor_scalar(
+                    grouped[LAST][:].rearrange("p (t d) -> p t d", d=4),
+                    picked_last[:].rearrange("p d t -> p t d"),
+                    1.0,
+                    0.0,
+                    MULT,
+                    ADD,
+                )
 
         def hand_over(c):
             up = keep.tile([P, H], F32, name=f"up_copy{ON_GPSIMD.index(c)}")

from contextlib import ExitStack

import concourse.mybir as mybir
from concourse.masks import make_identity

F32 = mybir.dt.float32
BF16 = mybir.dt.bfloat16
I32 = mybir.dt.int32
U32 = mybir.dt.uint32
U16 = mybir.dt.uint16
U8 = mybir.dt.uint8
FP8X4 = mybir.dt.float8_e4m3fn_x4
FP4X4 = mybir.dt.float4_e2m1fn_x4
GELU = mybir.ActivationFunctionType.Gelu_apprx_tanh
COPY = mybir.ActivationFunctionType.Copy
MULT = mybir.AluOpType.mult
ADD = mybir.AluOpType.add

P = 128
K, T, E, C, H, N = 512, 3072, 8, 256, 512, 128
S = E * C
SLICE = 512
SLICES = S // SLICE
CHUNKS = S // P
LAST = SLICES - 1
ON_VECTOR = (1024, 512, 896, 384)
CUTS = (0, 3, 6, 10, 13, 16)
SHARES = len(CUTS) - 1
UNIT_STARTS = sorted(set(range(0, CHUNKS, 2)) | set(CUTS))
UNITS = [list(range(first, last)) for first, last in zip(UNIT_STARTS[:-1], UNIT_STARTS[1:])]
RING = 4
AHEAD = 2 * RING
ON_GPSIMD = (AHEAD - 1,) + CUTS[-3:-1]
LEFT = 32
TURN = 8
STORE = 512
FIRST = 2
FLOPS = 2 * S * (2 * K * H + H * N)


def tile_moe_res_glu_gelu_kernel(
    tc, xT, xr, w1_words, w1_scales, w3_words, w3_scales, w2_words, w2_scales, gate, offs, out
):
    nc = tc.nc
    x_rows = xT.rearrange("(p d) t -> p d t", d=4)

    with ExitStack() as ctx:
        keep = ctx.enter_context(tc.tile_pool(name="keep", bufs=1))
        raw_pool = ctx.enter_context(tc.tile_pool(name="raw", bufs=1))
        psum = ctx.enter_context(tc.psum_pool(name="psum", bufs=1))

        offsets = keep.tile([P, S // 16], U16, name="offsets")
        rows = [raw_pool.tile([P, T + (H if d == 3 else 0)], F32, name=f"row{d}") for d in range(4)]
        behind_row3 = rows[3][:, T : T + H]
        picked = [[keep.tile([P, 2, SLICE], BF16, name=f"picked{u}_{s}") for s in range(LAST)] for u in range(2)]
        picked_last = keep.tile([P, 4, SLICE], BF16, name="picked_last")
        grouped = [keep.tile([P, 4 * SLICE], BF16, name=f"grouped{s}", align_bytes=64) for s in range(SLICES)]
        w1_codes = keep.tile([P, E * 2 * H], U8, name="w1_codes", align_bytes=64)
        w3_codes = keep.tile([P, E * 2 * H], U8, name="w3_codes", align_bytes=64)
        w2_codes = keep.tile([P, E * 2 * N], U8, name="w2_codes", align_bytes=64)
        w1_plane = [keep.tile([P, n * H], U8, name=f"w1_plane{n}", align_bytes=64) for n in (FIRST, E - FIRST)]
        w3_plane = [keep.tile([P, n * H], U8, name=f"w3_plane{n}", align_bytes=64) for n in (FIRST, E - FIRST)]
        w2_plane = keep.tile([P, E * N], U8, name="w2_plane", align_bytes=64)
        gates = keep.tile([P, S], F32, name="gates")
        residual = keep.tile([P, T], F32, name="residual")
        scattered = keep.tile([P, T], F32, name="scattered")
        identity = keep.tile([P, P], F32, name="identity")
        warm = keep.tile([P, 1], F32, name="warm")

        nc.vector.memset(warm[:], 0.0)
        nc.scalar.activation(warm[:], warm[:], GELU)
        for plane in w1_plane + w3_plane + [w2_plane]:
            nc.vector.memset(plane[:].bitcast(I32), 0)
        nc.vector.memset(scattered[:], 0.0)
        nc.vector.memset(behind_row3, 0.0)
        make_identity(nc, identity[:])

        def entries(first, last):
            return offsets[:, first // 16 : last // 16]

        def gather(d, first, last, on_vector):
            s, at = first // SLICE, first % SLICE
            row = picked_last[:, d] if s == LAST else picked[d // 2][s][:, d % 2]
            target = row[:, at : at + last - first]
            if on_vector:
                nc.vector.tensor_copy(target, rows[d][:].indirect(entries(first, last)))
            else:
                nc.scalar.activation(target, rows[d][:].indirect(entries(first, last)), COPY)

        def place(engine, u, s, first, last):
            engine.tensor_copy(
                out=grouped[s][:].rearrange("p (t d) -> p t d", d=4)[:, first:last, 2 * u : 2 * u + 2],
                in_=picked[u][s][:].rearrange("p d t -> p t d")[:, first:last, :],
            )

        for d in range(4):
            nc.sync.dma_start(out=rows[d][:, 0:T], in_=x_rows[:, d, :])
            if d == 0:
                nc.sync.dma_start(offsets[:], offs)
            cuts = sorted(set(range(0, S, SLICE)) | {ON_VECTOR[d]} | ({C, S - P} if d == 3 else {S}))
            for first, last in zip(cuts[:-1], cuts[1:]):
                gather(d, first, last, last <= ON_VECTOR[d])
            if d == 1:
                for s in range(LAST):
                    place(nc.vector, 0, s, 0, SLICE)

        def load_scales(plane, scales, e0, e1):
            for r in range(4):
                nc.sync.dma_start(
                    out=plane[r:P:32, :].bitcast(I32).rearrange("q (e i) -> q e i", e=e1 - e0),
                    in_=scales[e0:e1].rearrange("e s (q r) i -> r q (e s) i", r=4)[r].bitcast(I32),
                )

        def load_words(codes, words, e0, e1):
            wide = words.shape[3]
            nc.sync.dma_start(
                out=codes[:, e0 * wide : e1 * wide].bitcast(I32).rearrange("p (e b) -> p e b", e=e1 - e0),
                in_=words[e0:e1].rearrange("e s p b -> p (e s) b").bitcast(I32),
            )

        load_words(w1_codes, w1_words, 0, 2)
        load_scales(w1_plane[0], w1_scales, 0, FIRST)
        load_words(w3_codes, w3_words, 0, 2)
        load_scales(w3_plane[0], w3_scales, 0, FIRST)
        load_scales(w1_plane[1], w1_scales, FIRST, E)
        load_scales(w3_plane[1], w3_scales, FIRST, E)
        load_words(w1_codes, w1_words, 2, 4)
        load_words(w3_codes, w3_words, 2, 4)
        load_words(w1_codes, w1_words, 4, 6)
        load_words(w3_codes, w3_words, 4, 6)
        load_scales(w2_plane, w2_scales, 0, E)
        load_words(w2_codes, w2_words, 0, 4)
        nc.sync.dma_start(out=gates[:, 0:SLICE], in_=gate[:, 0:SLICE])
        load_words(w2_codes, w2_words, 4, E)
        load_words(w1_codes, w1_words, 6, E)
        load_words(w3_codes, w3_words, 6, E)
        nc.sync.dma_start(out=gates[:, SLICE:S], in_=gate[:, SLICE:S])
        nc.sync.dma_start(out=residual[:], in_=xr)

        x_codes = [keep.tile([P, SLICE], U32, name=f"x_codes{s}", align_bytes=64) for s in range(SLICES)]
        x_scales = [keep.tile([P, SLICE], U8, name=f"x_scales{s}", align_bytes=64) for s in range(LAST)]
        results = [keep.tile([P, SLICE], F32, name=f"results{k}") for k in range(SHARES)]
        a_banks, b_banks, acts, hiddens, turned, h_codes, h_scales, y_banks = ({} for kind in range(8))

        def units_of(k):
            return [u for u, unit in enumerate(UNITS) if CUTS[k] <= unit[0] < CUTS[k + 1]]

        banked = []
        for k in range(1, SHARES + 1):
            gelus = max(CUTS[min(k + 1, SHARES)], AHEAD)
            banked.extend(("gate", c) for c in range(gelus) if ("gate", c) not in banked)
            banked.extend(("group", u) for u in units_of(k - 1))
            if k >= 2:
                banked.append(("collect", k - 2))
        banked.append(("collect", SHARES - 1))
        held_chunk, holding_unit = ON_GPSIMD[0], units_of(0)[-1]
        steps = list(banked)
        for c in ON_GPSIMD:
            after = ("group", holding_unit) if c == held_chunk else ("gate", c)
            steps.insert(steps.index(after) + 1, ("hand", c))

        def bank_of(step):
            return psum.tile([P, H], F32, name=f"step{banked.index(step) % RING}")

        def first_product(bank, c, codes, plane):
            e, s, at = c // 2, c // 4, (c % 4) * P
            nc.tensor.matmul_mx(
                out=bank[:],
                lhsT=x_codes[s][:, at : at + P].bitcast(FP8X4),
                lhsT_scale=x_scales[s][:, at : at + P],
                rhs=codes[:, e * 2 * H : (e + 1) * 2 * H].bitcast(FP4X4),
                rhs_scale=plane[0][:, e * H : (e + 1) * H] if e < FIRST else plane[1][:, (e - FIRST) * H : (e - FIRST + 1) * H],
                start=True,
                stop=True,
            )

        def gate_product(c):
            a_banks[c] = bank_of(("gate", c))
            first_product(a_banks[c], c, w1_codes, w1_plane)

        def up_product(c):
            b_banks[c] = psum.tile([P, H], F32, name=f"up{c % RING}")
            first_product(b_banks[c], c, w3_codes, w3_plane)

        def from_bank(bank):
            return bank[:].rearrange("s (p u e) -> s u p e", u=2, e=2)

        def by_words(tile):
            return tile[:].rearrange("s (u p e) -> s u p e", u=2, e=2)

        def gate_chunk(c):
            acts[c] = behind_row3 if c == 1 else keep.tile([P, H], F32, name=f"act{c % TURN}")
            nc.scalar.activation(by_words(acts[c]), from_bank(a_banks[c]), GELU)
            if c not in ON_GPSIMD:
                hiddens[c] = keep.tile([P, H], BF16, name=f"hidden{c % TURN}", align_bytes=64)
                nc.vector.tensor_tensor(by_words(hiddens[c]), from_bank(b_banks[c]), by_words(acts[c]), MULT)
            if c == 1:
                gather(3, S - P, S, True)
                nc.gpsimd.tensor_scalar(
                    grouped[LAST][:].rearrange("p (t d) -> p t d", d=4),
                    picked_last[:].rearrange("p d t -> p t d"),
                    1.0,
                    0.0,
                    MULT,
                    ADD,
                )

        def hand_over(c):
            up = keep.tile([P, H], F32, name=f"up_copy{ON_GPSIMD.index(c)}")
            words = P - LEFT
            nc.scalar.copy(out=by_words(up)[:, 0], in_=from_bank(b_banks[c])[:, 0])
            nc.scalar.copy(out=by_words(up)[:, 1, 0:words], in_=from_bank(b_banks[c])[:, 1, 0:words])
            name = f"h_grouped{units_of(ON_GPSIMD.index(c))[-1]}"
            hiddens[c] = keep.tile([P, H], BF16, name=name, align_bytes=64)
            columns = 2 * (P + words)
            nc.gpsimd.tensor_tensor(hiddens[c][:, 0:columns], up[:, 0:columns], acts[c][:, 0:columns], MULT)
            nc.vector.tensor_tensor(
                by_words(hiddens[c])[:, 1, words:P],
                from_bank(b_banks[c])[:, 1, words:P],
                by_words(acts[c])[:, 1, words:P],
                MULT,
            )

        def turn(u):
            turned[u] = bank_of(("group", u))
            for n, c in enumerate(UNITS[u]):
                words = hiddens[c][:].bitcast(F32)
                for half in range(2):
                    at = (2 * n + half) * P
                    nc.tensor.transpose(turned[u][:, at : at + P], words[:, half * P : (half + 1) * P], identity[:])

        def quantise_tokens(s, first, last):
            nc.vector.quantize_mx(
                out=x_codes[s][:, first:last].bitcast(FP8X4),
                scales=x_scales[s][:, first:last],
                in_=grouped[s][:, 4 * first : 4 * last],
            )

        def group_unit(u):
            count = len(UNITS[u])
            h_grouped = keep.tile([P, 4 * P * count], BF16, name=f"h_grouped{u}", align_bytes=64)[:]
            nc.scalar.copy(
                out=h_grouped.bitcast(F32).rearrange("p (c s u) -> p c s u", c=count, u=2),
                in_=turned[u][:, 0 : 2 * P * count].rearrange("p (c u s) -> p c s u", c=count, u=2),
            )
            h_codes[u] = keep.tile([P, P * count], U32, name=f"h_codes{u}", align_bytes=64)
            h_scales[u] = keep.tile([P, P * count], U8, name=f"h_scales{u}", align_bytes=64)
            nc.vector.quantize_mx(out=h_codes[u][:].bitcast(FP8X4), scales=h_scales[u][:], in_=h_grouped)
            if u == holding_unit:
                x_scales.append(keep.tile([P, SLICE], U8, name="h_grouped0", align_bytes=64))
                quantise_tokens(LAST, 0, SLICE)

        def second_products(k):
            y_banks[k] = bank_of(("collect", k))
            for u in units_of(k):
                e, at = UNITS[u][0] // 2, (UNITS[u][0] - CUTS[k]) * P
                nc.tensor.matmul_mx(
                    out=y_banks[k][:, at : at + P * len(UNITS[u])],
                    lhsT=w2_codes[:, e * 2 * N : (e + 1) * 2 * N].bitcast(FP4X4),
                    lhsT_scale=w2_plane[:, e * N : (e + 1) * N],
                    rhs=h_codes[u][:].bitcast(FP8X4),
                    rhs_scale=h_scales[u][:],
                    start=True,
                    stop=True,
                )

        def put_back(k):
            first, last = CUTS[k] * P, CUTS[k + 1] * P
            nc.scalar.copy(out=results[k][:, 0 : last - first], in_=y_banks[k][:, 0 : last - first])
            nc.vector.tensor_tensor(
                scattered[:].indirect(entries(first, last)),
                results[k][:, 0 : last - first],
                gates[:, first:last],
                MULT,
            )

        place(nc.vector, 1, 0, 0, C)
        place(nc.vector, 1, 0, C, SLICE)
        quantise_tokens(0, 0, C)
        quantise_tokens(0, C, SLICE)
        for s in range(1, LAST):
            place(nc.vector, 1, s, 0, SLICE)
        for s in range(1, LAST):
            quantise_tokens(s, 0, SLICE)

        def inputs_written(step):
            kind, n = step
            if kind == "group":
                return all(c in hiddens for c in UNITS[n])
            if kind == "collect":
                return all(u in h_codes for u in units_of(n))
            return True

        fill = {"gate": gate_product, "group": turn, "collect": second_products}
        empty = {"gate": gate_chunk, "group": group_unit, "collect": put_back, "hand": hand_over}
        for kind, n in banked[:RING]:
            fill[kind](n)
        for c in range(RING):
            up_product(c)
        filled, emptied = RING, 0
        for kind, n in steps:
            empty[kind](n)
            emptied = emptied + (kind != "hand")
            while filled < len(banked) and filled < emptied + RING and inputs_written(banked[filled]):
                fill[banked[filled][0]](banked[filled][1])
                filled = filled + 1
            for c in range(RING, min(max(acts) + 3, CHUNKS)):
                if c not in b_banks and c - RING in hiddens:
                    up_product(c)

        cuts = [0] + list(range(STORE // 2, T, STORE)) + [T]
        for c0, c1 in zip(cuts[:-1], cuts[1:]):
            nc.vector.tensor_tensor(residual[:, c0:c1], residual[:, c0:c1], scattered[:, c0:c1], ADD)
            nc.sync.dma_start(out=out[:, c0:c1], in_=residual[:, c0:c1])
